import numpy as np
import ml_dtypes


def mxq(x, axis, fmt="e4m3"):
    dtype, down = {"e4m3": (ml_dtypes.float8_e4m3fn, 7), "e5m2": (ml_dtypes.float8_e5m2, 14)}[fmt]
    v = np.moveaxis(np.asarray(x, np.float32).astype(ml_dtypes.bfloat16).astype(np.float64), axis, -1)
    blocks = v.reshape(v.shape[:-1] + (-1, 32))
    amax = np.abs(blocks).max(-1, keepdims=True)
    byte = np.maximum(np.where(amax > 0, np.frexp(amax)[1] - 1 + 127, 0) - down, 1)
    scale = np.exp2(byte - 127.0)
    codes = (blocks / scale).astype(np.float32).astype(dtype).astype(np.float64)
    return np.moveaxis((codes * scale).reshape(v.shape), -1, axis)


WIDE = False


def mx_kscale(k):
    if not WIDE:
        return np.ones(k)
    levels = np.array([10, -10, 5, -5, 0])
    if k % 512:
        return np.exp2(np.random.permutation(np.resize(levels, k // 32))).repeat(32)
    a = np.empty((k // 512, 16))
    for p in range(k // 512):
        a[p, :8] = np.random.permutation(np.resize(levels, 8))
        for g in range(8):
            far = levels[np.abs(levels - a[p, g]) >= 10]
            a[p, g + 8] = far[np.random.randint(len(far))]
    return np.exp2(a.ravel()).repeat(32)


def f64(x):
    return np.asarray(x).astype(np.float64)


def striped(idx):
    return np.tile(idx.reshape(-1, 16).T, (8, 1)).astype(np.uint16)


def unstriped(offs):
    return offs[:16].T.reshape(-1).astype(np.int64)


def pack_weight(w):
    k, n = w.shape
    w = f64(np.asarray(w, np.float32).astype(ml_dtypes.bfloat16)).reshape(k // 32, 32, n)
    amax = np.abs(w).max(1)
    byte = np.clip(np.where(amax > 0, np.frexp(amax)[1] - 1 + 127 - 7, 1), 1, 254)
    scaled = (w * np.exp2(127.0 - byte)[:, None, :]).reshape(k, n).astype(np.float32)
    words = np.ascontiguousarray(scaled.reshape(k // 512, 128, 4, n).transpose(0, 1, 3, 2)).astype(ml_dtypes.float8_e4m3fn).view(np.uint8)
    return words, np.ascontiguousarray(byte.astype(np.uint8).reshape(k // 512, 16, n))


def unpack_weight(words, scales):
    g, p, n, _ = words.shape
    vals = np.ascontiguousarray(words).view(ml_dtypes.float8_e4m3fn).astype(np.float64) * np.repeat(np.exp2(scales.astype(np.float64) - 127.0), 8, axis=1)[..., None]
    return vals.transpose(0, 1, 3, 2).reshape(g * 512, n)


K, T, S, D, N, W = 512, 2048, 1024, 4, 256, 2048
P = 2 ** 7


def setup_inputs():
    n = np.random.standard_normal
    s = mx_kscale(K)[:, None]
    packed_xT = pack_weight(n((K, T)) * s)
    packed_eT = pack_weight(n((K, W)) * s)
    return {
        "x_words": packed_xT[0],
        "x_scales": packed_xT[1],
        "e_words": packed_eT[0],
        "e_scales": packed_eT[1],
        "w1": (n((K, N)) / np.sqrt(K) / s).astype(np.float32),
        "wb": (n((K, N)) / np.sqrt(K) / s).astype(np.float32),
        "mask": (np.tile(np.random.uniform(0.0, 1.0, S), (P, 1))).astype(np.float32),
        "tone": (np.random.uniform(0.5, 1.5, (N, 1))).astype(np.float32),
        "offs": striped(np.random.permutation(T)[:S]),
        "sec": striped(np.random.permutation(W)[:S]),
    }


def reference(x_words, x_scales, e_words, e_scales, w1, wb, mask, tone, offs, sec):
    xq = unpack_weight(x_words, x_scales)[:, unstriped(offs)]
    pa = mxq(f64(w1), 0, "e4m3").T @ xq
    ga = pa.reshape(len(pa), -1, D).mean(axis=2)
    la = pa - np.repeat(ga, D, axis=1)
    e_sec = unpack_weight(e_words, e_scales)[:, unstriped(sec)]
    pb = mxq(f64(wb), 0, "e4m3").T @ e_sec
    gb = pb.reshape(len(pb), -1, D).mean(axis=2)
    lb = pb - np.repeat(gb, D, axis=1)
    gm = f64(mask)[:1].reshape(len(f64(mask)[:1]), -1, D).mean(axis=2)
    low = f64(tone) * (gm * ga + (-1.0 * gm + 1.0) * gb)
    return np.maximum(la, lb) * (np.exp(-1.0 * np.abs(la - lb))) + np.repeat(low, D, axis=1)

@@ -1,0 +1,244 @@
+from contextlib import ExitStack
+
+import concourse.mybir as mybir
+
+K, T, S, D, N = 512, 2048, 1024, 4, 256
+FLOPS = 2 * 2 * K * N * S
+
+F32 = mybir.dt.float32
+BF16 = mybir.dt.bfloat16
+I32 = mybir.dt.int32
+U32 = mybir.dt.uint32
+U16 = mybir.dt.uint16
+U8 = mybir.dt.uint8
+FP8X4 = mybir.dt.float8_e4m3fn_x4
+ALU = mybir.AluOpType
+ACT = mybir.ActivationFunctionType
+
+P = 128
+PACK = 4
+HALVES = 2
+HALF = S // HALVES
+GROUPS = HALF // D
+TILES = N // P
+LIST_COLS = HALF // 16
+CLEAR_SPLIT = 1280
+
+
+def tile_picked_yblend_max_p_kernel(
+    tc, x_words, x_scales, e_words, e_scales, w1, wb, mask, tone, offs, sec, out
+):
+    nc = tc.nc
+    with ExitStack() as ctx:
+        keep = ctx.enter_context(tc.tile_pool(name="keep", bufs=1))
+        mm_psum = ctx.enter_context(tc.psum_pool(name="mm_psum", bufs=2))
+        sum_psum = ctx.enter_context(tc.psum_pool(name="sum_psum", bufs=2))
+        mean_psum = ctx.enter_context(tc.psum_pool(name="mean_psum", bufs=2))
+
+        late = ctx.enter_context(tc.tile_pool(name="late", bufs=1))
+        late_bytes = {"xw_win": 4 * T, "w1_raw": 4 * PACK * N, "ew_win": 4 * T, "wb_raw": 4 * PACK * N, "mask_t": 64, "tone_t": 64}
+        late_at, total = {}, 0
+        for name, size in late_bytes.items():
+            late_at[name] = total
+            total = total + size
+
+        def load_list(name, src):
+            t = keep.tile([P, S // 16], U16, name=name)
+            nc.sync.dma_start(t[:], src)
+            return t
+
+        def load_scales(t, src):
+            for q in range(4):
+                nc.sync.dma_start(
+                    t[32 * q : 32 * q + 4, :].bitcast(I32), src[0, 4 * q : 4 * q + 4, :].bitcast(I32)
+                )
+
+        def load_words(name, src):
+            t = late.tile([P, T], U32, name=name, align_bytes=64, offset=late_at[name])
+            nc.sync.dma_start(t[:].bitcast(I32), src[0].rearrange("p n t -> p (n t)").bitcast(I32))
+            return t
+
+        def load_weight(name, src):
+            t = late.tile([P, PACK, N], F32, name=name, offset=late_at[name])
+            nc.sync.dma_start(t[:], src.rearrange("(p j) n -> p j n", j=PACK))
+            return t
+
+        xs_win = keep.tile([P, T], U8, align_bytes=64)
+        es_win = keep.tile([P, T], U8, align_bytes=64)
+        nc.vector.memset(xs_win[:, :CLEAR_SPLIT].bitcast(I32), 0)
+        nc.gpsimd.memset(xs_win[:, CLEAR_SPLIT:].bitcast(I32), 0)
+        zeros = late.tile([P, total // 4], F32, offset=0)
+        nc.gpsimd.memset(zeros[:, :P], 0.0)
+        ident = keep.tile([P, P], F32)
+        nc.gpsimd.affine_select(
+            out=ident[:], in_=zeros[:, :P], compare_op=ALU.not_equal, fill=1.0, base=0,
+            pattern=[[-1, P]], channel_multiplier=1,
+        )
+        nc.gpsimd.memset(es_win[:].bitcast(I32), 0)
+
+        offs_t = load_list("offs_t", offs)
+        sec_t = load_list("sec_t", sec)
+        load_scales(xs_win, x_scales)
+        xw_win = load_words("xw_win", x_words)
+        w1_raw = load_weight("w1_raw", w1)
+        load_scales(es_win, e_scales)
+        ew_win = load_words("ew_win", e_words)
+        wb_raw = load_weight("wb_raw", wb)
+        mask_t = late.tile([P, HALVES, D], F32, offset=late_at["mask_t"])
+        nc.sync.dma_start(mask_t[:], mask[0].rearrange("(h v d) -> v h d", h=HALVES, d=D))
+        tone_t = late.tile([P, TILES], F32, offset=late_at["tone_t"])
+        with nc.allow_non_contiguous_dma(reason="one tone value for each channel's partition"):
+            nc.sync.dma_start(tone_t[:], tone.rearrange("(t p) o -> p (t o)", p=P))
+
+        warm = keep.tile([P, 1], F32)
+        nc.scalar.activation(warm[:], ident[:, 0:1], ACT.Exp)
+
+        def gather(name, win, lst, h, dtype):
+            t = keep.tile([P, HALF], dtype, name=f"{name}{h}", align_bytes=64)
+            nc.vector.tensor_copy(t[:], win[:].indirect(lst[:, h * LIST_COLS : (h + 1) * LIST_COLS]))
+            return t
+
+        def interleave(name, raw):
+            t = keep.tile([P, N, PACK], BF16, name=name, align_bytes=64)
+            nc.scalar.copy(t[:], raw[:].rearrange("p j n -> p n j"))
+            return t
+
+        def quantize(name, grouped):
+            codes = keep.tile([P, N], U32, name=name + "_codes", align_bytes=64)
+            scales = keep.tile([P, N], U8, name=name + "_scales", align_bytes=64)
+            nc.vector.quantize_mx(
+                out=codes[:].bitcast(FP8X4), scales=scales[:], in_=grouped[:].rearrange("p n j -> p (n j)")
+            )
+            return codes, scales
+
+        def product(name, w, words, scales, h):
+            res = []
+            for t in range(TILES):
+                acc = mm_psum.tile([P, HALF], F32, name="acc")
+                cols = slice(t * P, (t + 1) * P)
+                nc.tensor.matmul_mx(
+                    out=acc[:], lhsT=w[0][:, cols].bitcast(FP8X4), lhsT_scale=w[1][:, cols],
+                    rhs=words[:].bitcast(FP8X4), rhs_scale=scales[:], start=True, stop=True,
+                )
+                sb = keep.tile([P, 2, GROUPS, 2], F32, name=f"{name}_sb{h}{t}")
+                nc.scalar.copy(sb[:], acc[:].rearrange("p (v r e) -> p r v e", r=2, e=2))
+                res.append(sb)
+            return res
+
+        def group_sums(prods):
+            sums = sum_psum.tile([P, TILES, P], F32, name="sums")
+            for t in range(TILES):
+                for d in range(D):
+                    nc.tensor.matmul(
+                        sums[:, t, :], lhsT=prods[t][:, d // 2, :, d % 2], rhs=ident[:],
+                        is_transpose=True, start=(d == 0), stop=(d == D - 1),
+                    )
+            return sums
+
+        def scaled(name, sums, scale):
+            t = keep.tile([P, TILES, P], F32, name=name)
+            nc.scalar.activation(t[:], sums[:], ACT.Copy, scale=scale)
+            return t
+
+        def turn_back(dst, terms):
+            for t in range(TILES):
+                for i, term in enumerate(terms):
+                    nc.tensor.matmul(
+                        dst[:, t, :], lhsT=term[:, t, :], rhs=ident[:],
+                        is_transpose=True, start=(i == 0), stop=(i == len(terms) - 1),
+                    )
+
+        def spread(coarse):
+            return coarse.unsqueeze(2).to_broadcast([P, GROUPS, D])
+
+        def fine(name, prod, neg_mean):
+            t = keep.tile([P, HALF], F32, name=name)
+            nc.vector.tensor_tensor(
+                t[:].rearrange("p (v r e) -> p v r e", r=2, e=2),
+                prod[:].rearrange("p r v e -> p v r e"),
+                spread(neg_mean).rearrange("p v (r e) -> p v r e", e=2),
+                ALU.add,
+            )
+            return t
+
+        xs = [gather("xs", xs_win, offs_t, h, U8) for h in range(HALVES)]
+        xw = [gather("xw", xw_win, offs_t, h, U32) for h in range(HALVES)]
+        w1_q = quantize("w1", interleave("w1_g", w1_raw))
+        pa = [product("pa", w1_q, xw[h], xs[h], h) for h in range(HALVES)]
+
+        es, ew = [], []
+        es.append(gather("es", es_win, sec_t, 0, U8))
+        ew.append(gather("ew", ew_win, sec_t, 0, U32))
+        wb_q = quantize("wb", interleave("wb_g", wb_raw))
+        es.append(gather("es", es_win, sec_t, 1, U8))
+        ew.append(gather("ew", ew_win, sec_t, 1, U32))
+
+        share_a = keep.tile([P, HALVES], F32)
+        share_b = keep.tile([P, HALVES], F32)
+        mask_scaled = keep.tile([P, HALVES, D], F32)
+        for h in range(HALVES):
+            nc.scalar.activation(
+                mask_scaled[:, h, :], mask_t[:, h, :], ACT.Copy, scale=1.0 / (D * D), accum_out=share_a[:, h : h + 1]
+            )
+        nc.scalar.activation(share_b[:], share_a[:], ACT.Copy, scale=-1.0, bias=1.0 / D)
+
+        neg_ga, low_a = [], []
+        for h in range(HALVES):
+            sums = group_sums(pa[h])
+            turned = scaled(f"neg_ga_t{h}", sums, -1.0 / D)
+            low_a.append(scaled(f"low_a{h}", sums, share_a[:, h : h + 1]))
+            mean_a = mean_psum.tile([P, TILES, GROUPS], F32, name="mean_a")
+            turn_back(mean_a, [turned])
+            neg_ga.append(mean_a)
+
+        coarse_b = []
+        pb = []
+        for h in range(HALVES):
+            pb.append(product("pb", wb_q, ew[h], es[h], h))
+            sums = group_sums(pb[h])
+            turned = scaled(f"neg_gb_t{h}", sums, -1.0 / D)
+            low_b = scaled(f"low_b{h}", sums, share_b[:, h : h + 1])
+            cb = mean_psum.tile([P, 2, TILES, GROUPS], F32, name="coarse_b")
+            turn_back(cb[:, 0], [turned])
+            turn_back(cb[:, 1], [low_a[h], low_b])
+            coarse_b.append(cb)
+
+        la = [[fine(f"la{h}{t}", pa[h][t], neg_ga[h][:, t, :]) for t in range(TILES)] for h in range(HALVES)]
+
+        def front(h):
+            lb = [fine(f"lb{h}{t}", pb[h][t], coarse_b[h][:, 0, t, :]) for t in range(TILES)]
+            agree, larger = [], []
+            for t in range(TILES):
+                diff = keep.tile([P, HALF], F32, name=f"diff{h}{t}")
+                nc.vector.tensor_tensor(diff[:], la[h][t][:], lb[t][:], ALU.subtract)
+                dist = keep.tile([P, HALF], F32, name=f"dist{h}{t}")
+                nc.scalar.activation(dist[:], diff[:], ACT.Abs)
+                e = keep.tile([P, HALF], F32, name=f"agree{h}{t}")
+                nc.scalar.activation(e[:], dist[:], ACT.Exp, scale=-1.0)
+                agree.append(e)
+            for t in range(TILES):
+                m = keep.tile([P, HALF], F32, name=f"larger{h}{t}")
+                nc.vector.tensor_tensor(m[:], la[h][t][:], lb[t][:], ALU.max)
+                larger.append(m)
+            return agree, larger
+
+        def back(h, agree, larger):
+            detail = []
+            for t in range(TILES):
+                m = keep.tile([P, HALF], F32, name=f"detail{h}{t}")
+                nc.vector.tensor_tensor(m[:], larger[t][:], agree[t][:], ALU.mult)
+                detail.append(m)
+            for t in range(TILES):
+                res = keep.tile([P, HALF], F32, name=f"res{h}{t}")
+                nc.vector.scalar_tensor_tensor(
+                    res[:].rearrange("p (v d) -> p v d", d=D),
+                    spread(coarse_b[h][:, 1, t, :]),
+                    tone_t[:, t : t + 1],
+                    detail[t][:].rearrange("p (v d) -> p v d", d=D),
+                    ALU.mult, ALU.add,
+                )
+                nc.sync.dma_start(out[t * P : (t + 1) * P, h * HALF : (h + 1) * HALF], res[:])
+
+        fronts = [front(h) for h in range(HALVES)]
+        for h in range(HALVES):
+            back(h, *fronts[h])

@@ -31,16 +31,22 @@ def tile_picked_yblend_max_p_kernel(
     nc = tc.nc
     with ExitStack() as ctx:
         keep = ctx.enter_context(tc.tile_pool(name="keep", bufs=1))
-        mm_psum = ctx.enter_context(tc.psum_pool(name="mm_psum", bufs=2))
-        sum_psum = ctx.enter_context(tc.psum_pool(name="sum_psum", bufs=2))
-        mean_psum = ctx.enter_context(tc.psum_pool(name="mean_psum", bufs=2))
+        psum = ctx.enter_context(tc.psum_pool(name="psum", bufs=1))
+
+        def bank(i, name, shape):
+            return psum.tile(shape, F32, name=name, tag=f"bank{i}")
 
         late = ctx.enter_context(tc.tile_pool(name="late", bufs=1))
-        late_bytes = {"xw_win": 4 * T, "w1_raw": 4 * PACK * N, "ew_win": 4 * T, "wb_raw": 4 * PACK * N, "mask_t": 64, "tone_t": 64}
+        late_bytes = {"xw_win": 4 * T, "w1_raw": 4 * PACK * N, "es_win": T, "wb_raw": 4 * PACK * N, "ew_win": 4 * T + HALF, "mask_t": 64, "tone_t": 64}
+        reuse = ctx.enter_context(tc.tile_pool(name="reuse", bufs=1))
+        reuse_at = {"w1_g": 0, "es0": 0, "wb_g": 2048, "ew0": 1024, "ew1": 3072}
         late_at, total = {}, 0
         for name, size in late_bytes.items():
             late_at[name] = total
             total = total + size
+        late_at["es1"] = late_at["ew_win"]
+        for i, name in enumerate(["la00", "la01", "la10", "la11"]):
+            late_at[name] = late_at["ew_win"] + HALF + 4 * HALF * i
 
         def load_list(name, src):
             t = keep.tile([P, S // 16], U16, name=name)
@@ -64,7 +70,6 @@ def tile_picked_yblend_max_p_kernel(
             return t
 
         xs_win = keep.tile([P, T], U8, align_bytes=64)
-        es_win = keep.tile([P, T], U8, align_bytes=64)
         nc.vector.memset(xs_win[:, :CLEAR_SPLIT].bitcast(I32), 0)
         nc.gpsimd.memset(xs_win[:, CLEAR_SPLIT:].bitcast(I32), 0)
         zeros = late.tile([P, total // 4], F32, offset=0)
@@ -74,7 +79,12 @@ def tile_picked_yblend_max_p_kernel(
             out=ident[:], in_=zeros[:, :P], compare_op=ALU.not_equal, fill=1.0, base=0,
             pattern=[[-1, P]], channel_multiplier=1,
         )
+        es_win = late.tile([P, T], U8, align_bytes=64, offset=late_at["es_win"])
         nc.gpsimd.memset(es_win[:].bitcast(I32), 0)
+        warm_in = late.tile([P, (total - late_at["wb_raw"]) // 4], F32, offset=late_at["wb_raw"])
+        nc.gpsimd.memset(warm_in[:, 0:1], 0.0)
+        warm = keep.tile([P, 1], F32)
+        nc.scalar.activation(warm[:], warm_in[:, 0:1], ACT.Exp)
 
         offs_t = load_list("offs_t", offs)
         sec_t = load_list("sec_t", sec)
@@ -82,25 +92,28 @@ def tile_picked_yblend_max_p_kernel(
         xw_win = load_words("xw_win", x_words)
         w1_raw = load_weight("w1_raw", w1)
         load_scales(es_win, e_scales)
-        ew_win = load_words("ew_win", e_words)
         wb_raw = load_weight("wb_raw", wb)
+        ew_win = load_words("ew_win", e_words)
         mask_t = late.tile([P, HALVES, D], F32, offset=late_at["mask_t"])
         nc.sync.dma_start(mask_t[:], mask[0].rearrange("(h v d) -> v h d", h=HALVES, d=D))
         tone_t = late.tile([P, TILES], F32, offset=late_at["tone_t"])
         with nc.allow_non_contiguous_dma(reason="one tone value for each channel's partition"):
             nc.sync.dma_start(tone_t[:], tone.rearrange("(t p) o -> p (t o)", p=P))
 
-        warm = keep.tile([P, 1], F32)
-        nc.scalar.activation(warm[:], ident[:, 0:1], ACT.Exp)
 
         def gather(name, win, lst, h, dtype):
-            t = keep.tile([P, HALF], dtype, name=f"{name}{h}", align_bytes=64)
+            if f"{name}{h}" in reuse_at:
+                t = reuse.tile([P, HALF], dtype, name=f"{name}{h}", align_bytes=64, offset=reuse_at[f"{name}{h}"])
+            elif f"{name}{h}" in late_at:
+                t = late.tile([P, HALF], dtype, name=f"{name}{h}", align_bytes=64, offset=late_at[f"{name}{h}"])
+            else:
+                t = keep.tile([P, HALF], dtype, name=f"{name}{h}", align_bytes=64)
             nc.vector.tensor_copy(t[:], win[:].indirect(lst[:, h * LIST_COLS : (h + 1) * LIST_COLS]))
             return t
 
-        def interleave(name, raw):
-            t = keep.tile([P, N, PACK], BF16, name=name, align_bytes=64)
-            nc.scalar.copy(t[:], raw[:].rearrange("p j n -> p n j"))
+        def interleave(name, raw, sign):
+            t = reuse.tile([P, N, PACK], BF16, name=name, align_bytes=64, offset=reuse_at[name])
+            nc.scalar.activation(t[:], raw[:].rearrange("p j n -> p n j"), ACT.Copy, scale=sign)
             return t
 
         def quantize(name, grouped):
@@ -111,22 +124,29 @@ def tile_picked_yblend_max_p_kernel(
             )
             return codes, scales
 
-        def product(name, w, words, scales, h):
-            res = []
+        def product(name, terms, banks):
+            accs = []
             for t in range(TILES):
-                acc = mm_psum.tile([P, HALF], F32, name="acc")
+                acc = bank(banks[t], f"{name}{t}", [P, HALF])
                 cols = slice(t * P, (t + 1) * P)
-                nc.tensor.matmul_mx(
-                    out=acc[:], lhsT=w[0][:, cols].bitcast(FP8X4), lhsT_scale=w[1][:, cols],
-                    rhs=words[:].bitcast(FP8X4), rhs_scale=scales[:], start=True, stop=True,
-                )
-                sb = keep.tile([P, 2, GROUPS, 2], F32, name=f"{name}_sb{h}{t}")
+                for i, (w, words, scales) in enumerate(terms):
+                    nc.tensor.matmul_mx(
+                        out=acc[:], lhsT=w[0][:, cols].bitcast(FP8X4), lhsT_scale=w[1][:, cols],
+                        rhs=words[:].bitcast(FP8X4), rhs_scale=scales[:], start=(i == 0), stop=(i == len(terms) - 1),
+                    )
+                accs.append(acc)
+            return accs
+
+        def to_sbuf(name, accs):
+            res = []
+            for t, acc in enumerate(accs):
+                sb = keep.tile([P, 2, GROUPS, 2], F32, name=f"{name}{t}")
                 nc.scalar.copy(sb[:], acc[:].rearrange("p (v r e) -> p r v e", r=2, e=2))
                 res.append(sb)
             return res
 
-        def group_sums(prods):
-            sums = sum_psum.tile([P, TILES, P], F32, name="sums")
+        def group_sums(prods, at):
+            sums = bank(at, "sums", [P, TILES, P])
             for t in range(TILES):
                 for d in range(D):
                     nc.tensor.matmul(
@@ -152,7 +172,10 @@ def tile_picked_yblend_max_p_kernel(
             return coarse.unsqueeze(2).to_broadcast([P, GROUPS, D])
 
         def fine(name, prod, neg_mean):
-            t = keep.tile([P, HALF], F32, name=name)
+            if name in late_at:
+                t = late.tile([P, HALF], F32, name=name, offset=late_at[name])
+            else:
+                t = keep.tile([P, HALF], F32, name=name)
             nc.vector.tensor_tensor(
                 t[:].rearrange("p (v r e) -> p v r e", r=2, e=2),
                 prod[:].rearrange("p r v e -> p v r e"),
@@ -163,66 +186,76 @@ def tile_picked_yblend_max_p_kernel(
 
         xs = [gather("xs", xs_win, offs_t, h, U8) for h in range(HALVES)]
         xw = [gather("xw", xw_win, offs_t, h, U32) for h in range(HALVES)]
-        w1_q = quantize("w1", interleave("w1_g", w1_raw))
-        pa = [product("pa", w1_q, xw[h], xs[h], h) for h in range(HALVES)]
+        w1_q = quantize("w1", interleave("w1_g", w1_raw, 1.0))
+        wb_g = interleave("wb_g", wb_raw, -1.0)
+        pa = [to_sbuf(f"pa_sb{h}", product(f"pa{h}", [(w1_q, xw[h], xs[h])], [2 * h, 2 * h + 1])) for h in range(HALVES)]
 
-        es, ew = [], []
-        es.append(gather("es", es_win, sec_t, 0, U8))
-        ew.append(gather("ew", ew_win, sec_t, 0, U32))
-        wb_q = quantize("wb", interleave("wb_g", wb_raw))
-        es.append(gather("es", es_win, sec_t, 1, U8))
-        ew.append(gather("ew", ew_win, sec_t, 1, U32))
+        es0 = gather("es", es_win, sec_t, 0, U8)
+        wb_q = quantize("wb", wb_g)
+        ew = [gather("ew", ew_win, sec_t, h, U32) for h in range(HALVES)]
+        es1 = gather("es", es_win, sec_t, 1, U8)
 
-        share_a = keep.tile([P, HALVES], F32)
-        share_b = keep.tile([P, HALVES], F32)
-        mask_scaled = keep.tile([P, HALVES, D], F32)
+        means = [bank(6 + h, "means", [P, 2, TILES, GROUPS]) for h in range(HALVES)]
+
+        def neg_mean(name, prods, at, dst):
+            turned = scaled(name, group_sums(prods, at), -1.0 / D)
+            turn_back(dst, [turned])
+            return turned
+
+        neg_ga_t = [neg_mean(f"neg_ga_t{h}", pa[h], 4 + h, means[h][:, 0]) for h in range(HALVES)]
+        neg_pb = to_sbuf("pb_sb", product("pb", [(wb_q, ew[0], es0)], [3, 4]))
+        la = [[fine(f"la{h}{t}", pa[h][t], means[h][:, 0, t, :]) for t in range(TILES)] for h in range(HALVES)]
+        gb_t = neg_mean("gb_t", neg_pb, 0, means[0][:, 1])
+        pd = to_sbuf("pd_sb", product("pd", [(w1_q, xw[1], xs[1]), (wb_q, ew[1], es1)], [4, 0]))
+        neg_gd_t = neg_mean("neg_gd_t", pd, 1, means[1][:, 1])
+
+        neg_gm = keep.tile([P, HALVES], F32)
+        rest = keep.tile([P, HALVES], F32)
+        mask_scaled = reuse.tile([P, HALVES, D], F32, offset=reuse_at["ew0"])
         for h in range(HALVES):
             nc.scalar.activation(
-                mask_scaled[:, h, :], mask_t[:, h, :], ACT.Copy, scale=1.0 / (D * D), accum_out=share_a[:, h : h + 1]
+                mask_scaled[:, h, :], mask_t[:, h, :], ACT.Copy, scale=-1.0 / D, accum_out=neg_gm[:, h : h + 1]
             )
-        nc.scalar.activation(share_b[:], share_a[:], ACT.Copy, scale=-1.0, bias=1.0 / D)
+        nc.scalar.activation(rest[:, 0:1], neg_gm[:, 0:1], ACT.Copy, bias=1.0)
+        nc.scalar.activation(rest[:, 1:2], neg_gm[:, 1:2], ACT.Copy, scale=-1.0, bias=-1.0)
+        neg_tone = reuse.tile([P, TILES], F32, offset=reuse_at["ew0"] + 64)
+        nc.scalar.activation(neg_tone[:], tone_t[:], ACT.Copy, scale=-1.0)
+        low = bank(1, "low", [P, HALVES, TILES, GROUPS])
+        turn_back(low[:, 0], [scaled("low_a", neg_ga_t[0], neg_gm[:, 0:1]), scaled("low_b", gb_t, rest[:, 0:1])])
+        turn_back(low[:, 1], [neg_ga_t[1], scaled("low_d", neg_gd_t, rest[:, 1:2])])
+        tones = [tone_t, neg_tone]
 
-        neg_ga, low_a = [], []
-        for h in range(HALVES):
-            sums = group_sums(pa[h])
-            turned = scaled(f"neg_ga_t{h}", sums, -1.0 / D)
-            low_a.append(scaled(f"low_a{h}", sums, share_a[:, h : h + 1]))
-            mean_a = mean_psum.tile([P, TILES, GROUPS], F32, name="mean_a")
-            turn_back(mean_a, [turned])
-            neg_ga.append(mean_a)
+        def agreement(h, t, diff):
+            dist = keep.tile([P, HALF], F32, name=f"dist{h}{t}")
+            nc.scalar.activation(dist[:], diff[:], ACT.Abs)
+            e = keep.tile([P, HALF], F32, name=f"agree{h}{t}")
+            nc.scalar.activation(e[:], dist[:], ACT.Exp, scale=-1.0)
+            return e
 
-        coarse_b = []
-        pb = []
-        for h in range(HALVES):
-            pb.append(product("pb", wb_q, ew[h], es[h], h))
-            sums = group_sums(pb[h])
-            turned = scaled(f"neg_gb_t{h}", sums, -1.0 / D)
-            low_b = scaled(f"low_b{h}", sums, share_b[:, h : h + 1])
-            cb = mean_psum.tile([P, 2, TILES, GROUPS], F32, name="coarse_b")
-            turn_back(cb[:, 0], [turned])
-            turn_back(cb[:, 1], [low_a[h], low_b])
-            coarse_b.append(cb)
-
-        la = [[fine(f"la{h}{t}", pa[h][t], neg_ga[h][:, t, :]) for t in range(TILES)] for h in range(HALVES)]
-
-        def front(h):
-            lb = [fine(f"lb{h}{t}", pb[h][t], coarse_b[h][:, 0, t, :]) for t in range(TILES)]
+        def front0():
+            neg_lb = [fine(f"lb{t}", neg_pb[t], means[0][:, 1, t, :]) for t in range(TILES)]
             agree, larger = [], []
             for t in range(TILES):
-                diff = keep.tile([P, HALF], F32, name=f"diff{h}{t}")
-                nc.vector.tensor_tensor(diff[:], la[h][t][:], lb[t][:], ALU.subtract)
-                dist = keep.tile([P, HALF], F32, name=f"dist{h}{t}")
-                nc.scalar.activation(dist[:], diff[:], ACT.Abs)
-                e = keep.tile([P, HALF], F32, name=f"agree{h}{t}")
-                nc.scalar.activation(e[:], dist[:], ACT.Exp, scale=-1.0)
-                agree.append(e)
+                diff = keep.tile([P, HALF], F32, name=f"diff0{t}")
+                nc.vector.tensor_tensor(diff[:], la[0][t][:], neg_lb[t][:], ALU.add)
+                agree.append(agreement(0, t, diff))
             for t in range(TILES):
-                m = keep.tile([P, HALF], F32, name=f"larger{h}{t}")
-                nc.vector.tensor_tensor(m[:], la[h][t][:], lb[t][:], ALU.max)
+                m = keep.tile([P, HALF], F32, name=f"larger0{t}")
+                nc.vector.scalar_tensor_tensor(m[:], neg_lb[t][:], -1.0, la[0][t][:], ALU.mult, ALU.max)
                 larger.append(m)
-            return agree, larger
+            return agree, larger, ALU.add
 
-        def back(h, agree, larger):
+        def front1():
+            diff = [fine(f"diff1{t}", pd[t], means[1][:, 1, t, :]) for t in range(TILES)]
+            agree = [agreement(1, t, diff[t]) for t in range(TILES)]
+            larger = []
+            for t in range(TILES):
+                m = keep.tile([P, HALF], F32, name=f"larger1{t}")
+                nc.vector.scalar_tensor_tensor(m[:], diff[t][:], 0.0, la[1][t][:], ALU.min, ALU.subtract)
+                larger.append(m)
+            return agree, larger, ALU.subtract
+
+        def back(h, agree, larger, join):
             detail = []
             for t in range(TILES):
                 m = keep.tile([P, HALF], F32, name=f"detail{h}{t}")
@@ -232,13 +265,13 @@ def tile_picked_yblend_max_p_kernel(
                 res = keep.tile([P, HALF], F32, name=f"res{h}{t}")
                 nc.vector.scalar_tensor_tensor(
                     res[:].rearrange("p (v d) -> p v d", d=D),
-                    spread(coarse_b[h][:, 1, t, :]),
-                    tone_t[:, t : t + 1],
+                    spread(low[:, h, t, :]),
+                    tones[h][:, t : t + 1],
                     detail[t][:].rearrange("p (v d) -> p v d", d=D),
-                    ALU.mult, ALU.add,
+                    ALU.mult, join,
                 )
                 nc.sync.dma_start(out[t * P : (t + 1) * P, h * HALF : (h + 1) * HALF], res[:])
 
-        fronts = [front(h) for h in range(HALVES)]
+        fronts = [front0(), front1()]
         for h in range(HALVES):
             back(h, *fronts[h])

@@ -14,6 +14,7 @@ U8 = mybir.dt.uint8
 FP8X4 = mybir.dt.float8_e4m3fn_x4
 ALU = mybir.AluOpType
 ACT = mybir.ActivationFunctionType
+AXIS = mybir.AxisListType
 
 P = 128
 PACK = 4
@@ -37,7 +38,7 @@ def tile_picked_yblend_max_p_kernel(
             return psum.tile(shape, F32, name=name, tag=f"bank{i}")
 
         late = ctx.enter_context(tc.tile_pool(name="late", bufs=1))
-        late_bytes = {"xw_win": 4 * T, "w1_raw": 4 * PACK * N, "es_win": T, "wb_raw": 4 * PACK * N, "ew_win": 4 * T + HALF, "mask_t": 64, "tone_t": 64}
+        late_bytes = {"xw_win": 4 * T, "w1_raw": 4 * PACK * N, "wb_raw": 4 * PACK * N, "es_win": T, "ew_win": 4 * T, "mask_t": 64, "tone_t": 64}
         reuse = ctx.enter_context(tc.tile_pool(name="reuse", bufs=1))
         reuse_at = {"w1_g": 0, "es0": 0, "wb_g": 2048, "ew0": 1024, "ew1": 3072}
         late_at, total = {}, 0
@@ -45,8 +46,10 @@ def tile_picked_yblend_max_p_kernel(
             late_at[name] = total
             total = total + size
         late_at["es1"] = late_at["ew_win"]
+        late_at["pa_sb00"] = late_at["wb_raw"]
+        late_at["pa_sb01"] = late_at["wb_raw"] + 2048
         for i, name in enumerate(["la00", "la01", "la10", "la11"]):
-            late_at[name] = late_at["ew_win"] + HALF + 4 * HALF * i
+            late_at[name] = late_at["ew_win"] + 4 * HALF * i
 
         def load_list(name, src):
             t = keep.tile([P, S // 16], U16, name=name)
@@ -81,7 +84,7 @@ def tile_picked_yblend_max_p_kernel(
         )
         es_win = late.tile([P, T], U8, align_bytes=64, offset=late_at["es_win"])
         nc.gpsimd.memset(es_win[:].bitcast(I32), 0)
-        warm_in = late.tile([P, (total - late_at["wb_raw"]) // 4], F32, offset=late_at["wb_raw"])
+        warm_in = late.tile([P, (total - late_at["ew_win"]) // 4], F32, offset=late_at["ew_win"])
         nc.gpsimd.memset(warm_in[:, 0:1], 0.0)
         warm = keep.tile([P, 1], F32)
         nc.scalar.activation(warm[:], warm_in[:, 0:1], ACT.Exp)
@@ -91,8 +94,8 @@ def tile_picked_yblend_max_p_kernel(
         load_scales(xs_win, x_scales)
         xw_win = load_words("xw_win", x_words)
         w1_raw = load_weight("w1_raw", w1)
-        load_scales(es_win, e_scales)
         wb_raw = load_weight("wb_raw", wb)
+        load_scales(es_win, e_scales)
         ew_win = load_words("ew_win", e_words)
         mask_t = late.tile([P, HALVES, D], F32, offset=late_at["mask_t"])
         nc.sync.dma_start(mask_t[:], mask[0].rearrange("(h v d) -> v h d", h=HALVES, d=D))
@@ -117,7 +120,10 @@ def tile_picked_yblend_max_p_kernel(
             return t
 
         def quantize(name, grouped):
-            codes = keep.tile([P, N], U32, name=name + "_codes", align_bytes=64)
+            if name == "wb":
+                codes = late.tile([P, N], U32, name=name + "_codes", align_bytes=64, offset=late_at["es_win"])
+            else:
+                codes = keep.tile([P, N], U32, name=name + "_codes", align_bytes=64)
             scales = keep.tile([P, N], U8, name=name + "_scales", align_bytes=64)
             nc.vector.quantize_mx(
                 out=codes[:].bitcast(FP8X4), scales=scales[:], in_=grouped[:].rearrange("p n j -> p (n j)")
@@ -140,7 +146,10 @@ def tile_picked_yblend_max_p_kernel(
         def to_sbuf(name, accs):
             res = []
             for t, acc in enumerate(accs):
-                sb = keep.tile([P, 2, GROUPS, 2], F32, name=f"{name}{t}")
+                if f"{name}{t}" in late_at:
+                    sb = late.tile([P, 2, GROUPS, 2], F32, name=f"{name}{t}", offset=late_at[f"{name}{t}"])
+                else:
+                    sb = keep.tile([P, 2, GROUPS, 2], F32, name=f"{name}{t}")
                 nc.scalar.copy(sb[:], acc[:].rearrange("p (v r e) -> p r v e", r=2, e=2))
                 res.append(sb)
             return res
@@ -184,94 +193,109 @@ def tile_picked_yblend_max_p_kernel(
             )
             return t
 
-        xs = [gather("xs", xs_win, offs_t, h, U8) for h in range(HALVES)]
+        xs_all = keep.tile([P, S], U8, align_bytes=64)
+        nc.vector.tensor_copy(xs_all[:], xs_win[:].indirect(offs_t[:]))
+        xs = [xs_all[:, h * HALF : (h + 1) * HALF] for h in range(HALVES)]
         xw = [gather("xw", xw_win, offs_t, h, U32) for h in range(HALVES)]
         w1_q = quantize("w1", interleave("w1_g", w1_raw, 1.0))
         wb_g = interleave("wb_g", wb_raw, -1.0)
         pa = [to_sbuf(f"pa_sb{h}", product(f"pa{h}", [(w1_q, xw[h], xs[h])], [2 * h, 2 * h + 1])) for h in range(HALVES)]
-
-        es0 = gather("es", es_win, sec_t, 0, U8)
-        wb_q = quantize("wb", wb_g)
-        ew = [gather("ew", ew_win, sec_t, h, U32) for h in range(HALVES)]
-        es1 = gather("es", es_win, sec_t, 1, U8)
-
-        means = [bank(6 + h, "means", [P, 2, TILES, GROUPS]) for h in range(HALVES)]
+        neg_ga0 = bank(6, "neg_ga0", [P, TILES, GROUPS])
+        means1 = bank(7, "means1", [P, 2, TILES, GROUPS])
 
         def neg_mean(name, prods, at, dst):
             turned = scaled(name, group_sums(prods, at), -1.0 / D)
             turn_back(dst, [turned])
             return turned
 
-        neg_ga_t = [neg_mean(f"neg_ga_t{h}", pa[h], 4 + h, means[h][:, 0]) for h in range(HALVES)]
-        neg_pb = to_sbuf("pb_sb", product("pb", [(wb_q, ew[0], es0)], [3, 4]))
-        la = [[fine(f"la{h}{t}", pa[h][t], means[h][:, 0, t, :]) for t in range(TILES)] for h in range(HALVES)]
-        gb_t = neg_mean("gb_t", neg_pb, 0, means[0][:, 1])
-        pd = to_sbuf("pd_sb", product("pd", [(w1_q, xw[1], xs[1]), (wb_q, ew[1], es1)], [4, 0]))
-        neg_gd_t = neg_mean("neg_gd_t", pd, 1, means[1][:, 1])
+        neg_ga = [neg_ga0, means1[:, 0]]
+        neg_ga_t = [neg_mean(f"neg_ga_t{h}", pa[h], 4 + h, neg_ga[h]) for h in range(HALVES)]
+
+        es_all = reuse.tile([P, S], U8, align_bytes=64, offset=0)
+        nc.vector.tensor_copy(es_all[:], es_win[:].indirect(sec_t[:]))
+        es0, es1 = es_all[:, :HALF], es_all[:, HALF:]
+        wb_q = quantize("wb", wb_g)
+        ew = [gather("ew", ew_win, sec_t, h, U32) for h in (1, 0)][::-1]
+        neg_pb = to_sbuf("pb_sb", product("pb", [(wb_q, ew[1], es1)], [2, 3]))
+        pd = product("pd", [(wb_q, ew[0], es0), (w1_q, xw[0], xs[0])], [0, 1])
+        la = [[fine(f"la{h}{t}", pa[h][t], neg_ga[h][:, t, :]) for t in range(TILES)] for h in range(HALVES)]
+        gb_t = neg_mean("gb_t", neg_pb, 4, means1[:, 1])
+
+        def grouped(ap):
+            return ap.rearrange("p (v d) -> p v d", d=D)
+
+        def agreement(h, diffs):
+            dist = keep.tile([P, TILES, HALF], F32, name=f"dist{h}")
+            for t in range(TILES):
+                nc.scalar.activation(dist[:, t, :], diffs[t][:], ACT.Abs)
+            agree = keep.tile([P, TILES, HALF], F32, name=f"agree{h}")
+            nc.scalar.activation(agree[:], dist[:], ACT.Exp, scale=-1.0)
+            return agree
+
+        def detail(h, t, larger, agree):
+            m = keep.tile([P, HALF], F32, name=f"detail{h}{t}")
+            nc.vector.tensor_tensor(m[:], larger[t][:], agree[:, t, :], ALU.mult)
+            return m
+
+        def finish(h, t, fine_part, tone_col, join, pieces):
+            n = GROUPS // pieces
+            for i in range(pieces):
+                res = keep.tile([P, n, D], F32, name=f"res{h}{t}{i}")
+                coarse = low[:, h, t, i * n : (i + 1) * n].unsqueeze(2).to_broadcast([P, n, D])
+                nc.vector.scalar_tensor_tensor(
+                    res[:], coarse, tone_col[:, t : t + 1], grouped(fine_part[:])[:, i * n : (i + 1) * n, :], ALU.mult, join
+                )
+                first = h * HALF + i * n * D
+                nc.sync.dma_start(out[t * P : (t + 1) * P, first : first + n * D], res[:].rearrange("p v d -> p (v d)"))
+
+        sum_d = keep.tile([P, TILES, GROUPS], F32)
+        for t in range(TILES):
+            nc.vector.tensor_reduce(sum_d[:, t, :], grouped(pd[t][:]), AXIS.X, ALU.add)
+        diff0, larger0 = [], []
+        for t in range(TILES):
+            diff = keep.tile([P, HALF], F32, name=f"diff0{t}")
+            nc.vector.scalar_tensor_tensor(
+                grouped(diff[:]), spread(sum_d[:, t, :]), -1.0 / D, grouped(pd[t][:]), ALU.mult, ALU.add
+            )
+            diff0.append(diff)
+        agree0 = agreement(0, diff0)
+        for t in range(TILES):
+            m = keep.tile([P, HALF], F32, name=f"larger0{t}")
+            nc.vector.scalar_tensor_tensor(m[:], diff0[t][:], 0.0, la[0][t][:], ALU.min, ALU.subtract)
+            larger0.append(m)
 
         neg_gm = keep.tile([P, HALVES], F32)
         rest = keep.tile([P, HALVES], F32)
-        mask_scaled = reuse.tile([P, HALVES, D], F32, offset=reuse_at["ew0"])
+        mask_scaled = reuse.tile([P, HALVES, D], F32, offset=reuse_at["ew0"] + 1024)
         for h in range(HALVES):
             nc.scalar.activation(
                 mask_scaled[:, h, :], mask_t[:, h, :], ACT.Copy, scale=-1.0 / D, accum_out=neg_gm[:, h : h + 1]
             )
-        nc.scalar.activation(rest[:, 0:1], neg_gm[:, 0:1], ACT.Copy, bias=1.0)
-        nc.scalar.activation(rest[:, 1:2], neg_gm[:, 1:2], ACT.Copy, scale=-1.0, bias=-1.0)
-        neg_tone = reuse.tile([P, TILES], F32, offset=reuse_at["ew0"] + 64)
+        nc.scalar.activation(rest[:, 0:1], neg_gm[:, 0:1], ACT.Copy, scale=1.0 / D, bias=1.0 / D)
+        nc.scalar.activation(rest[:, 1:2], neg_gm[:, 1:2], ACT.Copy, bias=1.0)
+        neg_tone = reuse.tile([P, TILES], F32, offset=reuse_at["ew0"] + 1024 + 64)
         nc.scalar.activation(neg_tone[:], tone_t[:], ACT.Copy, scale=-1.0)
-        low = bank(1, "low", [P, HALVES, TILES, GROUPS])
-        turn_back(low[:, 0], [scaled("low_a", neg_ga_t[0], neg_gm[:, 0:1]), scaled("low_b", gb_t, rest[:, 0:1])])
-        turn_back(low[:, 1], [neg_ga_t[1], scaled("low_d", neg_gd_t, rest[:, 1:2])])
-        tones = [tone_t, neg_tone]
+        sum_d_t = bank(5, "sum_d_t", [P, TILES, P])
+        turn_back(sum_d_t, [sum_d])
+        low = bank(6, "low", [P, HALVES, TILES, GROUPS])
+        turn_back(low[:, 0], [neg_ga_t[0], scaled("low_d", sum_d_t, rest[:, 0:1])])
+        turn_back(low[:, 1], [scaled("low_a", neg_ga_t[1], neg_gm[:, 1:2]), scaled("low_b", gb_t, rest[:, 1:2])])
 
-        def agreement(h, t, diff):
-            dist = keep.tile([P, HALF], F32, name=f"dist{h}{t}")
-            nc.scalar.activation(dist[:], diff[:], ACT.Abs)
-            e = keep.tile([P, HALF], F32, name=f"agree{h}{t}")
-            nc.scalar.activation(e[:], dist[:], ACT.Exp, scale=-1.0)
-            return e
-
-        def front0():
-            neg_lb = [fine(f"lb{t}", neg_pb[t], means[0][:, 1, t, :]) for t in range(TILES)]
-            agree, larger = [], []
-            for t in range(TILES):
-                diff = keep.tile([P, HALF], F32, name=f"diff0{t}")
-                nc.vector.tensor_tensor(diff[:], la[0][t][:], neg_lb[t][:], ALU.add)
-                agree.append(agreement(0, t, diff))
-            for t in range(TILES):
-                m = keep.tile([P, HALF], F32, name=f"larger0{t}")
-                nc.vector.scalar_tensor_tensor(m[:], neg_lb[t][:], -1.0, la[0][t][:], ALU.mult, ALU.max)
-                larger.append(m)
-            return agree, larger, ALU.add
-
-        def front1():
-            diff = [fine(f"diff1{t}", pd[t], means[1][:, 1, t, :]) for t in range(TILES)]
-            agree = [agreement(1, t, diff[t]) for t in range(TILES)]
-            larger = []
-            for t in range(TILES):
-                m = keep.tile([P, HALF], F32, name=f"larger1{t}")
-                nc.vector.scalar_tensor_tensor(m[:], diff[t][:], 0.0, la[1][t][:], ALU.min, ALU.subtract)
-                larger.append(m)
-            return agree, larger, ALU.subtract
-
-        def back(h, agree, larger, join):
-            detail = []
-            for t in range(TILES):
-                m = keep.tile([P, HALF], F32, name=f"detail{h}{t}")
-                nc.vector.tensor_tensor(m[:], larger[t][:], agree[t][:], ALU.mult)
-                detail.append(m)
-            for t in range(TILES):
-                res = keep.tile([P, HALF], F32, name=f"res{h}{t}")
-                nc.vector.scalar_tensor_tensor(
-                    res[:].rearrange("p (v d) -> p v d", d=D),
-                    spread(low[:, h, t, :]),
-                    tones[h][:, t : t + 1],
-                    detail[t][:].rearrange("p (v d) -> p v d", d=D),
-                    ALU.mult, join,
-                )
-                nc.sync.dma_start(out[t * P : (t + 1) * P, h * HALF : (h + 1) * HALF], res[:])
-
-        fronts = [front0(), front1()]
-        for h in range(HALVES):
-            back(h, *fronts[h])
+        neg_lb = [fine(f"lb{t}", neg_pb[t], means1[:, 1, t, :]) for t in range(TILES)]
+        diff1, larger1 = [], []
+        for t in range(TILES):
+            diff = keep.tile([P, HALF], F32, name=f"diff1{t}")
+            nc.vector.tensor_tensor(diff[:], la[1][t][:], neg_lb[t][:], ALU.add)
+            diff1.append(diff)
+        agree1 = agreement(1, diff1)
+        for t in range(TILES):
+            m = keep.tile([P, HALF], F32, name=f"larger1{t}")
+            nc.vector.scalar_tensor_tensor(m[:], neg_lb[t][:], -1.0, la[1][t][:], ALU.mult, ALU.max)
+            larger1.append(m)
+        detail0 = [detail(0, t, larger0, agree0) for t in range(TILES)]
+        detail1 = []
+        for t in range(TILES):
+            finish(0, t, detail0[t], neg_tone, ALU.subtract, 1)
+            detail1.append(detail(1, t, larger1, agree1))
+        finish(1, 0, detail1[0], tone_t, ALU.add, 1)
+        finish(1, 1, detail1[1], tone_t, ALU.add, 2)

@@ -46,8 +46,6 @@ def tile_picked_yblend_max_p_kernel(
             late_at[name] = total
             total = total + size
         late_at["es1"] = late_at["ew_win"]
-        late_at["pa_sb00"] = late_at["wb_raw"]
-        late_at["pa_sb01"] = late_at["wb_raw"] + 2048
         for i, name in enumerate(["la00", "la01", "la10", "la11"]):
             late_at[name] = late_at["ew_win"] + 4 * HALF * i
 
@@ -143,14 +141,24 @@ def tile_picked_yblend_max_p_kernel(
                 accs.append(acc)
             return accs
 
-        def to_sbuf(name, accs):
+        def place(name, shape):
+            if name in late_at:
+                return late.tile(shape, F32, name=name, offset=late_at[name])
+            return keep.tile(shape, F32, name=name)
+
+        def dealt(name, accs):
             res = []
             for t, acc in enumerate(accs):
-                if f"{name}{t}" in late_at:
-                    sb = late.tile([P, 2, GROUPS, 2], F32, name=f"{name}{t}", offset=late_at[f"{name}{t}"])
-                else:
-                    sb = keep.tile([P, 2, GROUPS, 2], F32, name=f"{name}{t}")
-                nc.scalar.copy(sb[:], acc[:].rearrange("p (v r e) -> p r v e", r=2, e=2))
+                sb = place(f"{name}{t}", [P, D, GROUPS])
+                nc.scalar.copy(sb[:], acc[:].rearrange("p (v d) -> p d v", d=D))
+                res.append(sb)
+            return res
+
+        def plain(name, accs):
+            res = []
+            for t, acc in enumerate(accs):
+                sb = keep.tile([P, HALF], F32, name=f"{name}{t}")
+                nc.scalar.copy(sb[:], acc[:])
                 res.append(sb)
             return res
 
@@ -159,7 +167,7 @@ def tile_picked_yblend_max_p_kernel(
             for t in range(TILES):
                 for d in range(D):
                     nc.tensor.matmul(
-                        sums[:, t, :], lhsT=prods[t][:, d // 2, :, d % 2], rhs=ident[:],
+                        sums[:, t, :], lhsT=prods[t][:, d, :], rhs=ident[:],
                         is_transpose=True, start=(d == 0), stop=(d == D - 1),
                     )
             return sums
@@ -186,10 +194,7 @@ def tile_picked_yblend_max_p_kernel(
             else:
                 t = keep.tile([P, HALF], F32, name=name)
             nc.vector.tensor_tensor(
-                t[:].rearrange("p (v r e) -> p v r e", r=2, e=2),
-                prod[:].rearrange("p r v e -> p v r e"),
-                spread(neg_mean).rearrange("p v (r e) -> p v r e", e=2),
-                ALU.add,
+                t[:].rearrange("p (v d) -> p v d", d=D), prod[:].rearrange("p (v d) -> p v d", d=D), spread(neg_mean), ALU.add
             )
             return t
 
@@ -199,7 +204,8 @@ def tile_picked_yblend_max_p_kernel(
         xw = [gather("xw", xw_win, offs_t, h, U32) for h in range(HALVES)]
         w1_q = quantize("w1", interleave("w1_g", w1_raw, 1.0))
         wb_g = interleave("wb_g", wb_raw, -1.0)
-        pa = [to_sbuf(f"pa_sb{h}", product(f"pa{h}", [(w1_q, xw[h], xs[h])], [2 * h, 2 * h + 1])) for h in range(HALVES)]
+        pa_acc = [product(f"pa{h}", [(w1_q, xw[h], xs[h])], [2 * h, 2 * h + 1]) for h in range(HALVES)]
+        pa_dealt = [dealt(f"pa_sb{h}", pa_acc[h]) for h in range(HALVES)]
         neg_ga0 = bank(6, "neg_ga0", [P, TILES, GROUPS])
         means1 = bank(7, "means1", [P, 2, TILES, GROUPS])
 
@@ -209,17 +215,23 @@ def tile_picked_yblend_max_p_kernel(
             return turned
 
         neg_ga = [neg_ga0, means1[:, 0]]
-        neg_ga_t = [neg_mean(f"neg_ga_t{h}", pa[h], 4 + h, neg_ga[h]) for h in range(HALVES)]
+        neg_ga_t = [neg_mean("neg_ga_t0", pa_dealt[0], 4, neg_ga[0])]
+        pa = [plain("pa0", pa_acc[0])]
+        neg_ga_t.append(neg_mean("neg_ga_t1", pa_dealt[1], 5, neg_ga[1]))
+        pa.append(plain("pa1", pa_acc[1]))
 
         es_all = reuse.tile([P, S], U8, align_bytes=64, offset=0)
         nc.vector.tensor_copy(es_all[:], es_win[:].indirect(sec_t[:]))
         es0, es1 = es_all[:, :HALF], es_all[:, HALF:]
         wb_q = quantize("wb", wb_g)
         ew = [gather("ew", ew_win, sec_t, h, U32) for h in (1, 0)][::-1]
-        neg_pb = to_sbuf("pb_sb", product("pb", [(wb_q, ew[1], es1)], [2, 3]))
-        pd = product("pd", [(wb_q, ew[0], es0), (w1_q, xw[0], xs[0])], [0, 1])
+        neg_pb_acc = product("pb", [(wb_q, ew[1], es1)], [4, 5])
+
+        neg_pb_dealt = dealt("pb_sb", neg_pb_acc)
+        pd = product("pd", [(w1_q, xw[0], xs[0]), (wb_q, ew[0], es0)], [0, 1])
         la = [[fine(f"la{h}{t}", pa[h][t], neg_ga[h][:, t, :]) for t in range(TILES)] for h in range(HALVES)]
-        gb_t = neg_mean("gb_t", neg_pb, 4, means1[:, 1])
+        gb_t = neg_mean("gb_t", neg_pb_dealt, 2, means1[:, 1])
+        neg_pb = plain("pb", neg_pb_acc)
 
         def grouped(ap):
             return ap.rearrange("p (v d) -> p v d", d=D)
@@ -275,10 +287,10 @@ def tile_picked_yblend_max_p_kernel(
         nc.scalar.activation(rest[:, 1:2], neg_gm[:, 1:2], ACT.Copy, bias=1.0)
         neg_tone = reuse.tile([P, TILES], F32, offset=reuse_at["ew0"] + 1024 + 64)
         nc.scalar.activation(neg_tone[:], tone_t[:], ACT.Copy, scale=-1.0)
-        sum_d_t = bank(5, "sum_d_t", [P, TILES, P])
+        sum_d_t = bank(3, "sum_d_t", [P, TILES, P])
         turn_back(sum_d_t, [sum_d])
         low = bank(6, "low", [P, HALVES, TILES, GROUPS])
-        turn_back(low[:, 0], [neg_ga_t[0], scaled("low_d", sum_d_t, rest[:, 0:1])])
+        turn_back(low[:, 0], [scaled("low_d", sum_d_t, rest[:, 0:1]), neg_ga_t[0]])
         turn_back(low[:, 1], [scaled("low_a", neg_ga_t[1], neg_gm[:, 1:2]), scaled("low_b", gb_t, rest[:, 1:2])])
 
         neg_lb = [fine(f"lb{t}", neg_pb[t], means1[:, 1, t, :]) for t in range(TILES)]

@@ -18,12 +18,31 @@ AXIS = mybir.AxisListType
 
 P = 128
 PACK = 4
+QUADRANTS = 4
 HALVES = 2
 HALF = S // HALVES
 GROUPS = HALF // D
 TILES = N // P
 LIST_COLS = HALF // 16
-CLEAR_SPLIT = 1280
+LAST_PIECES = 2
+
+XW_AT = 0
+W1_AT = XW_AT + 4 * T
+WB_AT = W1_AT + 4 * PACK * N
+ES_AT = WB_AT + 4 * PACK * N
+EW_AT = ES_AT + T
+MASK_AT = EW_AT + 4 * T
+TONE_AT = MASK_AT + 64
+LOADS_END = TONE_AT + 64
+EW0_AT = LOADS_END
+
+PA_BANKS = [[0, 1], [2, 3]]
+PA_SUM_BANKS = [4, 5]
+NEG_GA0_BANK, MEANS1_BANK = 6, 7
+PB_BANKS = PA_BANKS[0]
+PD_BANKS = PA_SUM_BANKS
+PB_SUM_BANK = PA_BANKS[1][0]
+LOW_BANK = NEG_GA0_BANK
 
 
 def tile_picked_yblend_max_p_kernel(
@@ -32,99 +51,85 @@ def tile_picked_yblend_max_p_kernel(
     nc = tc.nc
     with ExitStack() as ctx:
         keep = ctx.enter_context(tc.tile_pool(name="keep", bufs=1))
+        shared = ctx.enter_context(tc.tile_pool(name="shared", bufs=1))
         psum = ctx.enter_context(tc.psum_pool(name="psum", bufs=1))
 
-        def bank(i, name, shape):
-            return psum.tile(shape, F32, name=name, tag=f"bank{i}")
-
-        late = ctx.enter_context(tc.tile_pool(name="late", bufs=1))
-        late_bytes = {"xw_win": 4 * T, "w1_raw": 4 * PACK * N, "wb_raw": 4 * PACK * N, "es_win": T, "ew_win": 4 * T, "mask_t": 64, "tone_t": 64}
-        reuse = ctx.enter_context(tc.tile_pool(name="reuse", bufs=1))
-        reuse_at = {"w1_g": 0, "es0": 0, "wb_g": 2048, "ew0": 1024, "ew1": 3072}
-        late_at, total = {}, 0
-        for name, size in late_bytes.items():
-            late_at[name] = total
-            total = total + size
-        late_at["es1"] = late_at["ew_win"]
-        for i, name in enumerate(["la00", "la01", "la10", "la11"]):
-            late_at[name] = late_at["ew_win"] + 4 * HALF * i
+        def bank(number, name, shape):
+            return psum.tile(shape, F32, name=name, tag=f"bank{number}")
 
         def load_list(name, src):
-            t = keep.tile([P, S // 16], U16, name=name)
-            nc.sync.dma_start(t[:], src)
-            return t
+            lst = keep.tile([P, S // 16], U16, name=name)
+            nc.sync.dma_start(lst[:], src)
+            return lst
 
-        def load_scales(t, src):
-            for q in range(4):
+        def load_scales(window, src):
+            for q in range(QUADRANTS):
                 nc.sync.dma_start(
-                    t[32 * q : 32 * q + 4, :].bitcast(I32), src[0, 4 * q : 4 * q + 4, :].bitcast(I32)
+                    window[32 * q : 32 * q + 4, :].bitcast(I32), src[0, 4 * q : 4 * q + 4, :].bitcast(I32)
                 )
 
-        def load_words(name, src):
-            t = late.tile([P, T], U32, name=name, align_bytes=64, offset=late_at[name])
-            nc.sync.dma_start(t[:].bitcast(I32), src[0].rearrange("p n t -> p (n t)").bitcast(I32))
-            return t
+        def load_words(name, src, at):
+            window = shared.tile([P, T], U32, name=name, align_bytes=64, offset=at)
+            nc.sync.dma_start(window[:].bitcast(I32), src[0].rearrange("p n t -> p (n t)").bitcast(I32))
+            return window
 
-        def load_weight(name, src):
-            t = late.tile([P, PACK, N], F32, name=name, offset=late_at[name])
-            nc.sync.dma_start(t[:], src.rearrange("(p j) n -> p j n", j=PACK))
-            return t
+        def load_weight(name, src, at):
+            raw = shared.tile([P, PACK, N], F32, name=name, offset=at)
+            nc.sync.dma_start(raw[:], src.rearrange("(p j) n -> p j n", j=PACK))
+            return raw
 
         xs_win = keep.tile([P, T], U8, align_bytes=64)
-        nc.vector.memset(xs_win[:, :CLEAR_SPLIT].bitcast(I32), 0)
-        nc.gpsimd.memset(xs_win[:, CLEAR_SPLIT:].bitcast(I32), 0)
-        zeros = late.tile([P, total // 4], F32, offset=0)
+        nc.vector.memset(xs_win[:].bitcast(I32), 0)
+        zeros = shared.tile([P, LOADS_END // 4], F32, offset=0)
         nc.gpsimd.memset(zeros[:, :P], 0.0)
         ident = keep.tile([P, P], F32)
         nc.gpsimd.affine_select(
             out=ident[:], in_=zeros[:, :P], compare_op=ALU.not_equal, fill=1.0, base=0,
             pattern=[[-1, P]], channel_multiplier=1,
         )
-        es_win = late.tile([P, T], U8, align_bytes=64, offset=late_at["es_win"])
+        es_win = shared.tile([P, T], U8, align_bytes=64, offset=ES_AT)
         nc.gpsimd.memset(es_win[:].bitcast(I32), 0)
-        warm_in = late.tile([P, (total - late_at["ew_win"]) // 4], F32, offset=late_at["ew_win"])
-        nc.gpsimd.memset(warm_in[:, 0:1], 0.0)
-        warm = keep.tile([P, 1], F32)
-        nc.scalar.activation(warm[:], warm_in[:, 0:1], ACT.Exp)
+
+        zero_col = shared.tile([P, (LOADS_END - EW_AT) // 4], F32, offset=EW_AT)
+        nc.gpsimd.memset(zero_col[:, 0:1], 0.0)
+        one = keep.tile([P, 1], F32)
+        nc.scalar.activation(one[:], zero_col[:, 0:1], ACT.Exp)
 
         offs_t = load_list("offs_t", offs)
         sec_t = load_list("sec_t", sec)
         load_scales(xs_win, x_scales)
-        xw_win = load_words("xw_win", x_words)
-        w1_raw = load_weight("w1_raw", w1)
-        wb_raw = load_weight("wb_raw", wb)
+        xw_win = load_words("xw_win", x_words, XW_AT)
+        w1_raw = load_weight("w1_raw", w1, W1_AT)
+        wb_raw = load_weight("wb_raw", wb, WB_AT)
         load_scales(es_win, e_scales)
-        ew_win = load_words("ew_win", e_words)
-        mask_t = late.tile([P, HALVES, D], F32, offset=late_at["mask_t"])
+        ew_win = load_words("ew_win", e_words, EW_AT)
+        mask_t = shared.tile([P, HALVES, D], F32, offset=MASK_AT)
         nc.sync.dma_start(mask_t[:], mask[0].rearrange("(h v d) -> v h d", h=HALVES, d=D))
-        tone_t = late.tile([P, TILES], F32, offset=late_at["tone_t"])
+        tone_t = shared.tile([P, TILES], F32, offset=TONE_AT)
         with nc.allow_non_contiguous_dma(reason="one tone value for each channel's partition"):
             nc.sync.dma_start(tone_t[:], tone.rearrange("(t p) o -> p (t o)", p=P))
 
+        def gather_scales(name, window, lst):
+            picked = keep.tile([P, S], U8, name=name, align_bytes=64)
+            nc.vector.tensor_copy(picked[:], window[:].indirect(lst[:]))
+            return [picked[:, h * HALF : (h + 1) * HALF] for h in range(HALVES)]
 
-        def gather(name, win, lst, h, dtype):
-            if f"{name}{h}" in reuse_at:
-                t = reuse.tile([P, HALF], dtype, name=f"{name}{h}", align_bytes=64, offset=reuse_at[f"{name}{h}"])
-            elif f"{name}{h}" in late_at:
-                t = late.tile([P, HALF], dtype, name=f"{name}{h}", align_bytes=64, offset=late_at[f"{name}{h}"])
-            else:
-                t = keep.tile([P, HALF], dtype, name=f"{name}{h}", align_bytes=64)
-            nc.vector.tensor_copy(t[:], win[:].indirect(lst[:, h * LIST_COLS : (h + 1) * LIST_COLS]))
-            return t
+        def gather_words(picked, window, lst, h):
+            nc.vector.tensor_copy(picked[:], window[:].indirect(lst[:, h * LIST_COLS : (h + 1) * LIST_COLS]))
+            return picked
+
+        def words_tile(name):
+            return keep.tile([P, HALF], U32, name=name, align_bytes=64)
 
         def interleave(name, raw, sign):
-            t = reuse.tile([P, N, PACK], BF16, name=name, align_bytes=64, offset=reuse_at[name])
-            nc.scalar.activation(t[:], raw[:].rearrange("p j n -> p n j"), ACT.Copy, scale=sign)
-            return t
+            side_by_side = keep.tile([P, N, PACK], BF16, name=name, align_bytes=64)
+            nc.scalar.activation(side_by_side[:], raw[:].rearrange("p j n -> p n j"), ACT.Copy, scale=sign)
+            return side_by_side
 
-        def quantize(name, grouped):
-            if name == "wb":
-                codes = late.tile([P, N], U32, name=name + "_codes", align_bytes=64, offset=late_at["es_win"])
-            else:
-                codes = keep.tile([P, N], U32, name=name + "_codes", align_bytes=64)
-            scales = keep.tile([P, N], U8, name=name + "_scales", align_bytes=64)
+        def quantize(name, side_by_side, codes):
+            scales = keep.tile([P, N], U8, name=name, align_bytes=64)
             nc.vector.quantize_mx(
-                out=codes[:].bitcast(FP8X4), scales=scales[:], in_=grouped[:].rearrange("p n j -> p (n j)")
+                out=codes[:].bitcast(FP8X4), scales=scales[:], in_=side_by_side[:].rearrange("p n j -> p (n j)")
             )
             return codes, scales
 
@@ -133,108 +138,99 @@ def tile_picked_yblend_max_p_kernel(
             for t in range(TILES):
                 acc = bank(banks[t], f"{name}{t}", [P, HALF])
                 cols = slice(t * P, (t + 1) * P)
-                for i, (w, words, scales) in enumerate(terms):
+                for i, ((w_codes, w_scales), words, scales) in enumerate(terms):
                     nc.tensor.matmul_mx(
-                        out=acc[:], lhsT=w[0][:, cols].bitcast(FP8X4), lhsT_scale=w[1][:, cols],
-                        rhs=words[:].bitcast(FP8X4), rhs_scale=scales[:], start=(i == 0), stop=(i == len(terms) - 1),
+                        out=acc[:], lhsT=w_codes[:, cols].bitcast(FP8X4), lhsT_scale=w_scales[:, cols],
+                        rhs=words[:].bitcast(FP8X4), rhs_scale=scales,
+                        start=(i == 0), stop=(i == len(terms) - 1),
                     )
                 accs.append(acc)
             return accs
 
-        def place(name, shape):
-            if name in late_at:
-                return late.tile(shape, F32, name=name, offset=late_at[name])
-            return keep.tile(shape, F32, name=name)
-
         def dealt(name, accs):
-            res = []
+            planes = []
             for t, acc in enumerate(accs):
-                sb = place(f"{name}{t}", [P, D, GROUPS])
+                sb = keep.tile([P, D, GROUPS], F32, name=f"{name}{t}")
                 nc.scalar.copy(sb[:], acc[:].rearrange("p (v d) -> p d v", d=D))
-                res.append(sb)
-            return res
+                planes.append(sb)
+            return planes
 
         def plain(name, accs):
-            res = []
+            rows = []
             for t, acc in enumerate(accs):
                 sb = keep.tile([P, HALF], F32, name=f"{name}{t}")
                 nc.scalar.copy(sb[:], acc[:])
-                res.append(sb)
-            return res
+                rows.append(sb)
+            return rows
 
-        def group_sums(prods, at):
-            sums = bank(at, "sums", [P, TILES, P])
+        def add_transposed(dst, terms):
+            for i, term in enumerate(terms):
+                nc.tensor.matmul(
+                    dst, lhsT=term, rhs=ident[:], is_transpose=True, start=(i == 0), stop=(i == len(terms) - 1)
+                )
+
+        def turn(dst, terms):
             for t in range(TILES):
-                for d in range(D):
-                    nc.tensor.matmul(
-                        sums[:, t, :], lhsT=prods[t][:, d, :], rhs=ident[:],
-                        is_transpose=True, start=(d == 0), stop=(d == D - 1),
-                    )
-            return sums
+                add_transposed(dst[:, t, :], [term[:, t, :] for term in terms])
 
-        def scaled(name, sums, scale):
-            t = keep.tile([P, TILES, P], F32, name=name)
-            nc.scalar.activation(t[:], sums[:], ACT.Copy, scale=scale)
-            return t
+        def scaled(name, src, scale):
+            dst = keep.tile([P, TILES, P], F32, name=name)
+            nc.scalar.activation(dst[:], src[:], ACT.Copy, scale=scale)
+            return dst
 
-        def turn_back(dst, terms):
+        def neg_mean(name, planes, sum_bank, dst):
+            sums = bank(sum_bank, name + "_sums", [P, TILES, P])
             for t in range(TILES):
-                for i, term in enumerate(terms):
-                    nc.tensor.matmul(
-                        dst[:, t, :], lhsT=term[:, t, :], rhs=ident[:],
-                        is_transpose=True, start=(i == 0), stop=(i == len(terms) - 1),
-                    )
-
-        def spread(coarse):
-            return coarse.unsqueeze(2).to_broadcast([P, GROUPS, D])
-
-        def fine(name, prod, neg_mean):
-            if name in late_at:
-                t = late.tile([P, HALF], F32, name=name, offset=late_at[name])
-            else:
-                t = keep.tile([P, HALF], F32, name=name)
-            nc.vector.tensor_tensor(
-                t[:].rearrange("p (v d) -> p v d", d=D), prod[:].rearrange("p (v d) -> p v d", d=D), spread(neg_mean), ALU.add
-            )
-            return t
-
-        xs_all = keep.tile([P, S], U8, align_bytes=64)
-        nc.vector.tensor_copy(xs_all[:], xs_win[:].indirect(offs_t[:]))
-        xs = [xs_all[:, h * HALF : (h + 1) * HALF] for h in range(HALVES)]
-        xw = [gather("xw", xw_win, offs_t, h, U32) for h in range(HALVES)]
-        w1_q = quantize("w1", interleave("w1_g", w1_raw, 1.0))
-        wb_g = interleave("wb_g", wb_raw, -1.0)
-        pa_acc = [product(f"pa{h}", [(w1_q, xw[h], xs[h])], [2 * h, 2 * h + 1]) for h in range(HALVES)]
-        pa_dealt = [dealt(f"pa_sb{h}", pa_acc[h]) for h in range(HALVES)]
-        neg_ga0 = bank(6, "neg_ga0", [P, TILES, GROUPS])
-        means1 = bank(7, "means1", [P, 2, TILES, GROUPS])
-
-        def neg_mean(name, prods, at, dst):
-            turned = scaled(name, group_sums(prods, at), -1.0 / D)
-            turn_back(dst, [turned])
+                add_transposed(sums[:, t, :], [planes[t][:, d, :] for d in range(D)])
+            turned = scaled(name, sums, -1.0 / D)
+            turn(dst, [turned])
             return turned
-
-        neg_ga = [neg_ga0, means1[:, 0]]
-        neg_ga_t = [neg_mean("neg_ga_t0", pa_dealt[0], 4, neg_ga[0])]
-        pa = [plain("pa0", pa_acc[0])]
-        neg_ga_t.append(neg_mean("neg_ga_t1", pa_dealt[1], 5, neg_ga[1]))
-        pa.append(plain("pa1", pa_acc[1]))
-
-        es_all = reuse.tile([P, S], U8, align_bytes=64, offset=0)
-        nc.vector.tensor_copy(es_all[:], es_win[:].indirect(sec_t[:]))
-        es0, es1 = es_all[:, :HALF], es_all[:, HALF:]
-        wb_q = quantize("wb", wb_g)
-        ew = [gather("ew", ew_win, sec_t, h, U32) for h in (1, 0)][::-1]
-        neg_pb_acc = product("pb", [(wb_q, ew[1], es1)], [4, 5])
-
-        neg_pb_dealt = dealt("pb_sb", neg_pb_acc)
-        pd = product("pd", [(w1_q, xw[0], xs[0]), (wb_q, ew[0], es0)], [0, 1])
-        la = [[fine(f"la{h}{t}", pa[h][t], neg_ga[h][:, t, :]) for t in range(TILES)] for h in range(HALVES)]
-        gb_t = neg_mean("gb_t", neg_pb_dealt, 2, means1[:, 1])
-        neg_pb = plain("pb", neg_pb_acc)
 
         def grouped(ap):
             return ap.rearrange("p (v d) -> p v d", d=D)
+
+        def spread(per_group):
+            return per_group.unsqueeze(2).to_broadcast([P, per_group.shape[1], D])
+
+        def fine(dst, prod, neg_means):
+            nc.vector.tensor_tensor(grouped(dst[:]), grouped(prod[:]), spread(neg_means), ALU.add)
+            return dst
+
+        def rows_tile(name):
+            return keep.tile([P, HALF], F32, name=name)
+
+        xs = gather_scales("xs", xs_win, offs_t)
+        xw = [gather_words(words_tile(f"xw{h}"), xw_win, offs_t, h) for h in range(HALVES)]
+        w1_codes = keep.tile([P, N], U32, align_bytes=64)
+        w1_q = quantize("w1_scales", interleave("w1_side", w1_raw, 1.0), w1_codes)
+        neg_wb_side = interleave("neg_wb_side", wb_raw, -1.0)
+        pa_acc = [product(f"pa{h}", [(w1_q, xw[h], xs[h])], PA_BANKS[h]) for h in range(HALVES)]
+        pa_dealt = [dealt(f"pa_dealt{h}", pa_acc[h]) for h in range(HALVES)]
+        neg_ga0 = bank(NEG_GA0_BANK, "neg_ga0", [P, TILES, GROUPS])
+        means1 = bank(MEANS1_BANK, "means1", [P, 2, TILES, GROUPS])
+        neg_ga = [neg_ga0, means1[:, 0]]
+        neg_ga_turned, pa = [], []
+        for h in range(HALVES):
+            neg_ga_turned.append(neg_mean(f"neg_ga_turned{h}", pa_dealt[h], PA_SUM_BANKS[h], neg_ga[h]))
+            pa.append(plain(f"pa_plain{h}", pa_acc[h]))
+
+        es = gather_scales("es", es_win, sec_t)
+        neg_wb_codes = shared.tile([P, N], U32, align_bytes=64, offset=ES_AT)
+        neg_wb_q = quantize("neg_wb_scales", neg_wb_side, neg_wb_codes)
+        ew1 = gather_words(words_tile("ew1"), ew_win, sec_t, 1)
+        ew0 = gather_words(shared.tile([P, HALF], U32, name="ew0", align_bytes=64, offset=EW0_AT), ew_win, sec_t, 0)
+        neg_pb_acc = product("neg_pb", [(neg_wb_q, ew1, es[1])], PB_BANKS)
+        neg_pb_dealt = dealt("neg_pb_dealt", neg_pb_acc)
+        pd = product("pd", [(w1_q, xw[0], xs[0]), (neg_wb_q, ew0, es[0])], PD_BANKS)
+
+        la = []
+        for h in range(HALVES):
+            la.append([])
+            for t in range(TILES):
+                dst = shared.tile([P, HALF], F32, name=f"la{h}{t}", offset=EW_AT + 4 * HALF * (TILES * h + t))
+                la[h].append(fine(dst, pa[h][t], neg_ga[h][:, t, :]))
+        gb_turned = neg_mean("gb_turned", neg_pb_dealt, PB_SUM_BANK, means1[:, 1])
+        neg_pb = plain("neg_pb_plain", neg_pb_acc)
 
         def agreement(h, diffs):
             dist = keep.tile([P, TILES, HALF], F32, name=f"dist{h}")
@@ -244,70 +240,67 @@ def tile_picked_yblend_max_p_kernel(
             nc.scalar.activation(agree[:], dist[:], ACT.Exp, scale=-1.0)
             return agree
 
-        def detail(h, t, larger, agree):
-            m = keep.tile([P, HALF], F32, name=f"detail{h}{t}")
-            nc.vector.tensor_tensor(m[:], larger[t][:], agree[:, t, :], ALU.mult)
-            return m
-
-        def finish(h, t, fine_part, tone_col, join, pieces):
-            n = GROUPS // pieces
-            for i in range(pieces):
-                res = keep.tile([P, n, D], F32, name=f"res{h}{t}{i}")
-                coarse = low[:, h, t, i * n : (i + 1) * n].unsqueeze(2).to_broadcast([P, n, D])
-                nc.vector.scalar_tensor_tensor(
-                    res[:], coarse, tone_col[:, t : t + 1], grouped(fine_part[:])[:, i * n : (i + 1) * n, :], ALU.mult, join
-                )
-                first = h * HALF + i * n * D
-                nc.sync.dma_start(out[t * P : (t + 1) * P, first : first + n * D], res[:].rearrange("p v d -> p (v d)"))
-
-        sum_d = keep.tile([P, TILES, GROUPS], F32)
+        pd_sums = keep.tile([P, TILES, GROUPS], F32)
         for t in range(TILES):
-            nc.vector.tensor_reduce(sum_d[:, t, :], grouped(pd[t][:]), AXIS.X, ALU.add)
-        diff0, larger0 = [], []
+            nc.vector.tensor_reduce(pd_sums[:, t, :], grouped(pd[t][:]), AXIS.X, ALU.add)
+        diff0 = [rows_tile(f"diff0{t}") for t in range(TILES)]
         for t in range(TILES):
-            diff = keep.tile([P, HALF], F32, name=f"diff0{t}")
             nc.vector.scalar_tensor_tensor(
-                grouped(diff[:]), spread(sum_d[:, t, :]), -1.0 / D, grouped(pd[t][:]), ALU.mult, ALU.add
+                grouped(diff0[t][:]), spread(pd_sums[:, t, :]), -1.0 / D, grouped(pd[t][:]), ALU.mult, ALU.add
             )
-            diff0.append(diff)
         agree0 = agreement(0, diff0)
+        neg_larger0 = [rows_tile(f"neg_larger0{t}") for t in range(TILES)]
         for t in range(TILES):
-            m = keep.tile([P, HALF], F32, name=f"larger0{t}")
-            nc.vector.scalar_tensor_tensor(m[:], diff0[t][:], 0.0, la[0][t][:], ALU.min, ALU.subtract)
-            larger0.append(m)
+            nc.vector.scalar_tensor_tensor(neg_larger0[t][:], diff0[t][:], 0.0, la[0][t][:], ALU.min, ALU.subtract)
 
         neg_gm = keep.tile([P, HALVES], F32)
-        rest = keep.tile([P, HALVES], F32)
-        mask_scaled = reuse.tile([P, HALVES, D], F32, offset=reuse_at["ew0"] + 1024)
+        mask_scaled = shared.tile([P, HALVES, D], F32, offset=EW0_AT)
         for h in range(HALVES):
             nc.scalar.activation(
                 mask_scaled[:, h, :], mask_t[:, h, :], ACT.Copy, scale=-1.0 / D, accum_out=neg_gm[:, h : h + 1]
             )
-        nc.scalar.activation(rest[:, 0:1], neg_gm[:, 0:1], ACT.Copy, scale=1.0 / D, bias=1.0 / D)
-        nc.scalar.activation(rest[:, 1:2], neg_gm[:, 1:2], ACT.Copy, bias=1.0)
-        neg_tone = reuse.tile([P, TILES], F32, offset=reuse_at["ew0"] + 1024 + 64)
+        pd_share = keep.tile([P, 1], F32)
+        nc.scalar.activation(pd_share[:], neg_gm[:, 0:1], ACT.Copy, scale=1.0 / D, bias=1.0 / D)
+        gb_share = keep.tile([P, 1], F32)
+        nc.scalar.activation(gb_share[:], neg_gm[:, 1:2], ACT.Identity, bias=one[:])
+        neg_tone = shared.tile([P, TILES], F32, offset=EW0_AT + 64)
         nc.scalar.activation(neg_tone[:], tone_t[:], ACT.Copy, scale=-1.0)
-        sum_d_t = bank(3, "sum_d_t", [P, TILES, P])
-        turn_back(sum_d_t, [sum_d])
-        low = bank(6, "low", [P, HALVES, TILES, GROUPS])
-        turn_back(low[:, 0], [scaled("low_d", sum_d_t, rest[:, 0:1]), neg_ga_t[0]])
-        turn_back(low[:, 1], [scaled("low_a", neg_ga_t[1], neg_gm[:, 1:2]), scaled("low_b", gb_t, rest[:, 1:2])])
+        pd_sums_turned = bank(PB_SUM_BANK, "pd_sums_turned", [P, TILES, P])
+        turn(pd_sums_turned, [pd_sums])
+        low = bank(LOW_BANK, "low", [P, HALVES, TILES, GROUPS])
+        turn(low[:, 0], [scaled("pd_part", pd_sums_turned, pd_share[:]), neg_ga_turned[0]])
+        turn(low[:, 1], [scaled("ga_part", neg_ga_turned[1], neg_gm[:, 1:2]), scaled("gb_part", gb_turned, gb_share[:])])
 
-        neg_lb = [fine(f"lb{t}", neg_pb[t], means1[:, 1, t, :]) for t in range(TILES)]
-        diff1, larger1 = [], []
+        neg_lb = [fine(rows_tile(f"neg_lb{t}"), neg_pb[t], means1[:, 1, t, :]) for t in range(TILES)]
+        diff1 = [rows_tile(f"diff1{t}") for t in range(TILES)]
         for t in range(TILES):
-            diff = keep.tile([P, HALF], F32, name=f"diff1{t}")
-            nc.vector.tensor_tensor(diff[:], la[1][t][:], neg_lb[t][:], ALU.add)
-            diff1.append(diff)
+            nc.vector.tensor_tensor(diff1[t][:], la[1][t][:], neg_lb[t][:], ALU.add)
         agree1 = agreement(1, diff1)
+        larger1 = [rows_tile(f"larger1{t}") for t in range(TILES)]
         for t in range(TILES):
-            m = keep.tile([P, HALF], F32, name=f"larger1{t}")
-            nc.vector.scalar_tensor_tensor(m[:], neg_lb[t][:], -1.0, la[1][t][:], ALU.mult, ALU.max)
-            larger1.append(m)
-        detail0 = [detail(0, t, larger0, agree0) for t in range(TILES)]
+            nc.vector.scalar_tensor_tensor(larger1[t][:], neg_lb[t][:], -1.0, la[1][t][:], ALU.mult, ALU.max)
+
+        def weighted(name, larger, agree):
+            dst = rows_tile(name)
+            nc.vector.tensor_tensor(dst[:], larger[:], agree, ALU.mult)
+            return dst
+
+        def finish(h, t, detail, tone_cols, join, pieces):
+            n = GROUPS // pieces
+            for i in range(pieces):
+                groups = slice(i * n, (i + 1) * n)
+                res = keep.tile([P, n, D], F32, name=f"res{h}{t}{i}")
+                nc.vector.scalar_tensor_tensor(
+                    res[:], spread(low[:, h, t, groups]), tone_cols[:, t : t + 1], grouped(detail[:])[:, groups, :],
+                    ALU.mult, join,
+                )
+                first = h * HALF + i * n * D
+                nc.sync.dma_start(out[t * P : (t + 1) * P, first : first + n * D], res[:].rearrange("p v d -> p (v d)"))
+
+        neg_detail0 = [weighted(f"neg_detail0{t}", neg_larger0[t], agree0[:, t, :]) for t in range(TILES)]
         detail1 = []
         for t in range(TILES):
-            finish(0, t, detail0[t], neg_tone, ALU.subtract, 1)
-            detail1.append(detail(1, t, larger1, agree1))
-        finish(1, 0, detail1[0], tone_t, ALU.add, 1)
-        finish(1, 1, detail1[1], tone_t, ALU.add, 2)
+            finish(0, t, neg_detail0[t], neg_tone, ALU.subtract, 1)
+            detail1.append(weighted(f"detail1{t}", larger1[t], agree1[:, t, :]))
+        for t in range(TILES):
+            finish(1, t, detail1[t], tone_t, ALU.add, LAST_PIECES if t == TILES - 1 else 1)

from contextlib import ExitStack

import concourse.mybir as mybir

K, T, S, D, N = 512, 2048, 1024, 4, 256
FLOPS = 2 * 2 * K * N * S

F32 = mybir.dt.float32
BF16 = mybir.dt.bfloat16
I32 = mybir.dt.int32
U32 = mybir.dt.uint32
U16 = mybir.dt.uint16
U8 = mybir.dt.uint8
FP8X4 = mybir.dt.float8_e4m3fn_x4
ALU = mybir.AluOpType
ACT = mybir.ActivationFunctionType
AXIS = mybir.AxisListType

P = 128
PACK = 4
QUADRANTS = 4
HALVES = 2
HALF = S // HALVES
GROUPS = HALF // D
TILES = N // P
LIST_COLS = HALF // 16
LAST_PIECES = 2

XW_AT = 0
W1_AT = XW_AT + 4 * T
WB_AT = W1_AT + 4 * PACK * N
ES_AT = WB_AT + 4 * PACK * N
EW_AT = ES_AT + T
MASK_AT = EW_AT + 4 * T
TONE_AT = MASK_AT + 64
LOADS_END = TONE_AT + 64
EW0_AT = LOADS_END

PA_BANKS = [[0, 1], [2, 3]]
PA_SUM_BANKS = [4, 5]
NEG_GA0_BANK, MEANS1_BANK = 6, 7
PB_BANKS = PA_BANKS[0]
PD_BANKS = PA_SUM_BANKS
PB_SUM_BANK = PA_BANKS[1][0]
LOW_BANK = NEG_GA0_BANK


def tile_picked_yblend_max_p_kernel(
    tc, x_words, x_scales, e_words, e_scales, w1, wb, mask, tone, offs, sec, out
):
    nc = tc.nc
    with ExitStack() as ctx:
        keep = ctx.enter_context(tc.tile_pool(name="keep", bufs=1))
        shared = ctx.enter_context(tc.tile_pool(name="shared", bufs=1))
        psum = ctx.enter_context(tc.psum_pool(name="psum", bufs=1))

        def bank(number, name, shape):
            return psum.tile(shape, F32, name=name, tag=f"bank{number}")

        def load_list(name, src):
            lst = keep.tile([P, S // 16], U16, name=name)
            nc.sync.dma_start(lst[:], src)
            return lst

        def load_scales(window, src):
            for q in range(QUADRANTS):
                nc.sync.dma_start(
                    window[32 * q : 32 * q + 4, :].bitcast(I32), src[0, 4 * q : 4 * q + 4, :].bitcast(I32)
                )

        def load_words(name, src, at):
            window = shared.tile([P, T], U32, name=name, align_bytes=64, offset=at)
            nc.sync.dma_start(window[:].bitcast(I32), src[0].rearrange("p n t -> p (n t)").bitcast(I32))
            return window

        def load_weight(name, src, at):
            raw = shared.tile([P, PACK, N], F32, name=name, offset=at)
            nc.sync.dma_start(raw[:], src.rearrange("(p j) n -> p j n", j=PACK))
            return raw

        xs_win = keep.tile([P, T], U8, align_bytes=64)
        nc.vector.memset(xs_win[:].bitcast(I32), 0)
        zeros = shared.tile([P, LOADS_END // 4], F32, offset=0)
        nc.gpsimd.memset(zeros[:, :P], 0.0)
        ident = keep.tile([P, P], F32)
        nc.gpsimd.affine_select(
            out=ident[:], in_=zeros[:, :P], compare_op=ALU.not_equal, fill=1.0, base=0,
            pattern=[[-1, P]], channel_multiplier=1,
        )
        es_win = shared.tile([P, T], U8, align_bytes=64, offset=ES_AT)
        nc.gpsimd.memset(es_win[:].bitcast(I32), 0)

        zero_col = shared.tile([P, (LOADS_END - EW_AT) // 4], F32, offset=EW_AT)
        nc.gpsimd.memset(zero_col[:, 0:1], 0.0)
        one = keep.tile([P, 1], F32)
        nc.scalar.activation(one[:], zero_col[:, 0:1], ACT.Exp)

        offs_t = load_list("offs_t", offs)
        sec_t = load_list("sec_t", sec)
        load_scales(xs_win, x_scales)
        xw_win = load_words("xw_win", x_words, XW_AT)
        w1_raw = load_weight("w1_raw", w1, W1_AT)
        wb_raw = load_weight("wb_raw", wb, WB_AT)
        load_scales(es_win, e_scales)
        ew_win = load_words("ew_win", e_words, EW_AT)
        mask_t = shared.tile([P, HALVES, D], F32, offset=MASK_AT)
        nc.sync.dma_start(mask_t[:], mask[0].rearrange("(h v d) -> v h d", h=HALVES, d=D))
        tone_t = shared.tile([P, TILES], F32, offset=TONE_AT)
        with nc.allow_non_contiguous_dma(reason="one tone value for each channel's partition"):
            nc.sync.dma_start(tone_t[:], tone.rearrange("(t p) o -> p (t o)", p=P))

        def gather_scales(name, window, lst):
            picked = keep.tile([P, S], U8, name=name, align_bytes=64)
            nc.vector.tensor_copy(picked[:], window[:].indirect(lst[:]))
            return [picked[:, h * HALF : (h + 1) * HALF] for h in range(HALVES)]

        def gather_words(picked, window, lst, h):
            nc.vector.tensor_copy(picked[:], window[:].indirect(lst[:, h * LIST_COLS : (h + 1) * LIST_COLS]))
            return picked

        def words_tile(name):
            return keep.tile([P, HALF], U32, name=name, align_bytes=64)

        def interleave(name, raw, sign):
            side_by_side = keep.tile([P, N, PACK], BF16, name=name, align_bytes=64)
            nc.scalar.activation(side_by_side[:], raw[:].rearrange("p j n -> p n j"), ACT.Copy, scale=sign)
            return side_by_side

        def quantize(name, side_by_side, codes):
            scales = keep.tile([P, N], U8, name=name, align_bytes=64)
            nc.vector.quantize_mx(
                out=codes[:].bitcast(FP8X4), scales=scales[:], in_=side_by_side[:].rearrange("p n j -> p (n j)")
            )
            return codes, scales

        def product(name, terms, banks):
            accs = []
            for t in range(TILES):
                acc = bank(banks[t], f"{name}{t}", [P, HALF])
                cols = slice(t * P, (t + 1) * P)
                for i, ((w_codes, w_scales), words, scales) in enumerate(terms):
                    nc.tensor.matmul_mx(
                        out=acc[:], lhsT=w_codes[:, cols].bitcast(FP8X4), lhsT_scale=w_scales[:, cols],
                        rhs=words[:].bitcast(FP8X4), rhs_scale=scales,
                        start=(i == 0), stop=(i == len(terms) - 1),
                    )
                accs.append(acc)
            return accs

        def dealt(name, accs):
            planes = []
            for t, acc in enumerate(accs):
                sb = keep.tile([P, D, GROUPS], F32, name=f"{name}{t}")
                nc.scalar.copy(sb[:], acc[:].rearrange("p (v d) -> p d v", d=D))
                planes.append(sb)
            return planes

        def plain(name, accs):
            rows = []
            for t, acc in enumerate(accs):
                sb = keep.tile([P, HALF], F32, name=f"{name}{t}")
                nc.scalar.copy(sb[:], acc[:])
                rows.append(sb)
            return rows

        def add_transposed(dst, terms):
            for i, term in enumerate(terms):
                nc.tensor.matmul(
                    dst, lhsT=term, rhs=ident[:], is_transpose=True, start=(i == 0), stop=(i == len(terms) - 1)
                )

        def turn(dst, terms):
            for t in range(TILES):
                add_transposed(dst[:, t, :], [term[:, t, :] for term in terms])

        def scaled(name, src, scale):
            dst = keep.tile([P, TILES, P], F32, name=name)
            nc.scalar.activation(dst[:], src[:], ACT.Copy, scale=scale)
            return dst

        def neg_mean(name, planes, sum_bank, dst):
            sums = bank(sum_bank, name + "_sums", [P, TILES, P])
            for t in range(TILES):
                add_transposed(sums[:, t, :], [planes[t][:, d, :] for d in range(D)])
            turned = scaled(name, sums, -1.0 / D)
            turn(dst, [turned])
            return turned

        def grouped(ap):
            return ap.rearrange("p (v d) -> p v d", d=D)

        def spread(per_group):
            return per_group.unsqueeze(2).to_broadcast([P, per_group.shape[1], D])

        def fine(dst, prod, neg_means):
            nc.vector.tensor_tensor(grouped(dst[:]), grouped(prod[:]), spread(neg_means), ALU.add)
            return dst

        def rows_tile(name):
            return keep.tile([P, HALF], F32, name=name)

        xs = gather_scales("xs", xs_win, offs_t)
        xw = [gather_words(words_tile(f"xw{h}"), xw_win, offs_t, h) for h in range(HALVES)]
        w1_codes = keep.tile([P, N], U32, align_bytes=64)
        w1_q = quantize("w1_scales", interleave("w1_side", w1_raw, 1.0), w1_codes)
        neg_wb_side = interleave("neg_wb_side", wb_raw, -1.0)
        pa_acc = [product(f"pa{h}", [(w1_q, xw[h], xs[h])], PA_BANKS[h]) for h in range(HALVES)]
        pa_dealt = [dealt(f"pa_dealt{h}", pa_acc[h]) for h in range(HALVES)]
        neg_ga0 = bank(NEG_GA0_BANK, "neg_ga0", [P, TILES, GROUPS])
        means1 = bank(MEANS1_BANK, "means1", [P, 2, TILES, GROUPS])
        neg_ga = [neg_ga0, means1[:, 0]]
        neg_ga_turned, pa = [], []
        for h in range(HALVES):
            neg_ga_turned.append(neg_mean(f"neg_ga_turned{h}", pa_dealt[h], PA_SUM_BANKS[h], neg_ga[h]))
            pa.append(plain(f"pa_plain{h}", pa_acc[h]))

        es = gather_scales("es", es_win, sec_t)
        neg_wb_codes = shared.tile([P, N], U32, align_bytes=64, offset=ES_AT)
        neg_wb_q = quantize("neg_wb_scales", neg_wb_side, neg_wb_codes)
        ew1 = gather_words(words_tile("ew1"), ew_win, sec_t, 1)
        ew0 = gather_words(shared.tile([P, HALF], U32, name="ew0", align_bytes=64, offset=EW0_AT), ew_win, sec_t, 0)
        neg_pb_acc = product("neg_pb", [(neg_wb_q, ew1, es[1])], PB_BANKS)
        neg_pb_dealt = dealt("neg_pb_dealt", neg_pb_acc)
        pd = product("pd", [(w1_q, xw[0], xs[0]), (neg_wb_q, ew0, es[0])], PD_BANKS)

        la = []
        for h in range(HALVES):
            la.append([])
            for t in range(TILES):
                dst = shared.tile([P, HALF], F32, name=f"la{h}{t}", offset=EW_AT + 4 * HALF * (TILES * h + t))
                la[h].append(fine(dst, pa[h][t], neg_ga[h][:, t, :]))
        gb_turned = neg_mean("gb_turned", neg_pb_dealt, PB_SUM_BANK, means1[:, 1])
        neg_pb = plain("neg_pb_plain", neg_pb_acc)

        def agreement(h, diffs):
            dist = keep.tile([P, TILES, HALF], F32, name=f"dist{h}")
            for t in range(TILES):
                nc.scalar.activation(dist[:, t, :], diffs[t][:], ACT.Abs)
            agree = keep.tile([P, TILES, HALF], F32, name=f"agree{h}")
            nc.scalar.activation(agree[:], dist[:], ACT.Exp, scale=-1.0)
            return agree

        pd_sums = keep.tile([P, TILES, GROUPS], F32)
        for t in range(TILES):
            nc.vector.tensor_reduce(pd_sums[:, t, :], grouped(pd[t][:]), AXIS.X, ALU.add)
        diff0 = [rows_tile(f"diff0{t}") for t in range(TILES)]
        for t in range(TILES):
            nc.vector.scalar_tensor_tensor(
                grouped(diff0[t][:]), spread(pd_sums[:, t, :]), -1.0 / D, grouped(pd[t][:]), ALU.mult, ALU.add
            )
        agree0 = agreement(0, diff0)
        neg_larger0 = [rows_tile(f"neg_larger0{t}") for t in range(TILES)]
        for t in range(TILES):
            nc.vector.scalar_tensor_tensor(neg_larger0[t][:], diff0[t][:], 0.0, la[0][t][:], ALU.min, ALU.subtract)

        neg_gm = keep.tile([P, HALVES], F32)
        mask_scaled = shared.tile([P, HALVES, D], F32, offset=EW0_AT)
        for h in range(HALVES):
            nc.scalar.activation(
                mask_scaled[:, h, :], mask_t[:, h, :], ACT.Copy, scale=-1.0 / D, accum_out=neg_gm[:, h : h + 1]
            )
        pd_share = keep.tile([P, 1], F32)
        nc.scalar.activation(pd_share[:], neg_gm[:, 0:1], ACT.Copy, scale=1.0 / D, bias=1.0 / D)
        gb_share = keep.tile([P, 1], F32)
        nc.scalar.activation(gb_share[:], neg_gm[:, 1:2], ACT.Identity, bias=one[:])
        neg_tone = shared.tile([P, TILES], F32, offset=EW0_AT + 64)
        nc.scalar.activation(neg_tone[:], tone_t[:], ACT.Copy, scale=-1.0)
        pd_sums_turned = bank(PB_SUM_BANK, "pd_sums_turned", [P, TILES, P])
        turn(pd_sums_turned, [pd_sums])
        low = bank(LOW_BANK, "low", [P, HALVES, TILES, GROUPS])
        turn(low[:, 0], [scaled("pd_part", pd_sums_turned, pd_share[:]), neg_ga_turned[0]])
        turn(low[:, 1], [scaled("ga_part", neg_ga_turned[1], neg_gm[:, 1:2]), scaled("gb_part", gb_turned, gb_share[:])])

        neg_lb = [fine(rows_tile(f"neg_lb{t}"), neg_pb[t], means1[:, 1, t, :]) for t in range(TILES)]
        diff1 = [rows_tile(f"diff1{t}") for t in range(TILES)]
        for t in range(TILES):
            nc.vector.tensor_tensor(diff1[t][:], la[1][t][:], neg_lb[t][:], ALU.add)
        agree1 = agreement(1, diff1)
        larger1 = [rows_tile(f"larger1{t}") for t in range(TILES)]
        for t in range(TILES):
            nc.vector.scalar_tensor_tensor(larger1[t][:], neg_lb[t][:], -1.0, la[1][t][:], ALU.mult, ALU.max)

        def weighted(name, larger, agree):
            dst = rows_tile(name)
            nc.vector.tensor_tensor(dst[:], larger[:], agree, ALU.mult)
            return dst

        def finish(h, t, detail, tone_cols, join, pieces):
            n = GROUPS // pieces
            for i in range(pieces):
                groups = slice(i * n, (i + 1) * n)
                res = keep.tile([P, n, D], F32, name=f"res{h}{t}{i}")
                nc.vector.scalar_tensor_tensor(
                    res[:], spread(low[:, h, t, groups]), tone_cols[:, t : t + 1], grouped(detail[:])[:, groups, :],
                    ALU.mult, join,
                )
                first = h * HALF + i * n * D
                nc.sync.dma_start(out[t * P : (t + 1) * P, first : first + n * D], res[:].rearrange("p v d -> p (v d)"))

        neg_detail0 = [weighted(f"neg_detail0{t}", neg_larger0[t], agree0[:, t, :]) for t in range(TILES)]
        detail1 = []
        for t in range(TILES):
            finish(0, t, neg_detail0[t], neg_tone, ALU.subtract, 1)
            detail1.append(weighted(f"detail1{t}", larger1[t], agree1[:, t, :]))
        for t in range(TILES):
            finish(1, t, detail1[t], tone_t, ALU.add, LAST_PIECES if t == TILES - 1 else 1)
